import numpy as np, ml_dtypes
CORES = [66,74,82,90,194,202,210,218]
N = 8
T, EL, CAP, CAPP = 2048, 2, 960, 256
E = N * EL
def entries(a): return a.T.reshape(-1)
def pack(v, P): return np.ascontiguousarray(np.asarray(v, np.int32).reshape(-1, P).T)
def lists(rng, how):
    if how == "uniform": return {"ex": np.stack([pack(rng.permutation(np.repeat(np.arange(E), CAPP))[:T], 16) for r in range(N)])}
    R = np.arange(N)[:, None]; c = rng.permutation(E); C = np.zeros((N, E), np.int64)
    if how == "bands":
        a = c % N; C = CAPP * ((R >= a) & (R <= a + CAP // CAPP)); C[a, np.arange(E)] = np.where(c < N, CAPP, rng.integers(1, CAPP + 1, E))
    if how == "full":
        g = T // CAPP; C[:, c[:g]] = CAPP; C[:, c[:g // 2]] = rng.integers(CAPP // 2, CAPP + 1, (N, g // 2))
    if how in ("skew", "sorted"):
        V = np.full((N, 3), CAP // N); V[:, 0] = rng.integers(2, CAP // N + 1, N); h = rng.integers(1, N - 2); V[h, 0] = 0; V[h + 1, 0] = 1; V[rng.integers(N), 1:] += CAP % N; V[rng.integers(N), 2] += 1
        W = rng.random((N, E)) ** 4 + 1e-9; W[:, c[:3]] = 0
        C = np.minimum(((T - T // 8 - V.sum(axis=1, keepdims=True)) * W / W.sum(axis=1, keepdims=True)).astype(np.int64), CAPP); C[:, c[:3]] = V
    if how == "thin":
        C = rng.integers(0, CAP // N + 1, (N, E)); C[1] = 1; C[[0, N // 2, N - 1]] = 0
    X = np.stack([rng.permutation(np.concatenate([np.repeat(np.arange(E), C[r]), np.full(T - C[r].sum(), -1)])) for r in range(N)])
    if how == "sorted": X = np.sort(X, axis=1); X[1::2] = X[1::2, ::-1].copy()
    return {"ex": np.stack([pack(v, 16) for v in X])}
def blank(d):
    for r in range(0, N, 2):
        u, i = np.unique(entries(d["ex"][r])[::-1], return_index=True); d["x"][r][:, T - 1 - i[u >= 0]] = 0
def setup_inputs(rng):
    return dict({"x": rng.standard_normal((N, 128, T), dtype=np.float32).astype(ml_dtypes.bfloat16)}, **lists(rng, "uniform"))
def setup_inputs_bands(rng):
    d = setup_inputs(rng); d.update(lists(rng, "bands"))
    for k in ("x",): d[k] = (d[k].astype(np.float32) * 1048576.0).astype(d[k].dtype)
    blank(d)
    return d
def setup_inputs_full(rng):
    d = setup_inputs(rng); d.update(lists(rng, "full"))
    for k in ("x",): d[k] = (d[k].astype(np.float32) * (1 / 1024.0)).astype(d[k].dtype)
    blank(d)
    return d
def setup_inputs_skew(rng):
    d = setup_inputs(rng); d.update(lists(rng, "skew"))
    blank(d)
    return d
def setup_inputs_sorted(rng):
    d = setup_inputs(rng); d.update(lists(rng, "sorted"))
    blank(d)
    return d
def setup_inputs_thin(rng):
    d = setup_inputs(rng); d.update(lists(rng, "thin"))
    blank(d)
    return d
def check_inputs(x):
    bad = []
    if x["ex"].min() < -1 or x["ex"].max() >= E: bad.append("ex out of range")
    if max(int(np.bincount(entries(a)[entries(a) >= 0], minlength=E).max()) for a in x["ex"]) > CAPP: bad.append("more than CAPP tokens of one rank choose one expert")
    return bad
def reference(x, ex):
    X = np.concatenate(list(x), axis=1); e = np.concatenate([entries(a) for a in ex])
    k = np.nonzero(e >= 0)[0]; o = k[np.argsort(e[k], kind="stable")]; s = e[o]
    p = np.arange(len(o)) - np.searchsorted(s, s)
    Y = np.zeros((128, E * CAP), x.dtype); m = p < CAP; Y[:, CAP * s[m] + p[m]] = X[:, o[m]]
    return {"y": np.stack([Y[:, EL * CAP * r:EL * CAP * (r + 1)] for r in range(N)])}

@@ -1,0 +1,306 @@
+from concourse.bass import DstId, RemoteDMATransfer
+from concourse.mybir import AluOpType as Op, AxisListType, ActivationFunctionType as Fn
+
+BF, F32, I32, U16 = "bfloat16", "float32", "int32", "uint16"
+SCRATCH = {
+    "exall": ("dram", [8, 128, 16], I32),
+    "e16": ("sbuf", [128, 128], I32), "e16b": ("sbuf", [128, 128], BF),
+    "e8": ("sbuf", [128, 16], I32), "e8b": ("sbuf", [128, 16], BF),
+    "xs": ("sbuf", [128, 2048], BF), "sb": ("sbuf", [128, 2048], BF),
+    "land": ("sbuf", [128, 4112], BF), "yt": ("sbuf", [128, 1920], BF),
+    "pcol": ("sbuf", [128, 1], I32), "gi": ("sbuf", [128, 1], I32), "ii": ("sbuf", [128, 1], I32), "kp": ("sbuf", [128, 1], I32),
+    "gcol": ("sbuf", [128, 1], F32), "icol": ("sbuf", [128, 1], F32), "pf": ("sbuf", [128, 1], F32), "kpf": ("sbuf", [128, 1], F32),
+    "ka": ("sbuf", [128, 1], F32), "kcol": ("sbuf", [128, 1], F32), "kw": ("sbuf", [128, 1], F32),
+    "w0": ("sbuf", [128, 1], F32), "w1": ("sbuf", [128, 1], F32), "wg": ("sbuf", [128, 1], F32), "ww": ("sbuf", [128, 1], F32),
+    "rowi": ("sbuf", [128, 144], BF), "rowg": ("sbuf", [128, 128], BF), "row": ("sbuf", [128, 256], BF),
+    "r16": ("sbuf", [128, 128], BF), "lneg": ("sbuf", [128, 128], BF), "lpos": ("sbuf", [128, 16], BF),
+    "mb": ("sbuf", [128, 128], BF), "mg": ("sbuf", [128, 128], BF), "ma": ("sbuf", [128, 128], BF),
+    "zw": ("sbuf", [128, 240], BF), "zk": ("sbuf", [128, 240], BF), "zl": ("sbuf", [128, 144], BF),
+    "dm": ("sbuf", [128, 128], BF), "rh": ("sbuf", [128, 1024], BF),
+    "oh": ("sbuf", [128, 128], BF), "sc": ("sbuf", [128, 136], BF), "pr": ("sbuf", [128, 128], BF),
+    "offs": ("sbuf", [128, 16], U16), "vals": ("sbuf", [128, 256], BF), "win": ("sbuf", [128, 2304], BF),
+    "offx": ("sbuf", [128, 128], U16),
+    "allex": ("sbuf", [128, 128], I32), "eq0": ("sbuf", [128, 128], F32), "eq1": ("sbuf", [128, 128], F32),
+    "cnt": ("sbuf", [128, 2], F32), "rbs": ("sbuf", [128, 128], F32), "rb": ("sbuf", [128, 128], F32), "rd": ("sbuf", [128, 128], F32),
+    "pl": ("sbuf", [128, 60], F32), "pc": ("sbuf", [128, 120], F32), "wc": ("sbuf", [128, 2], F32), "uu": ("sbuf", [128, 120], F32),
+    "roff": ("sbuf", [128, 120], U16),
+    "pb": ("psum", [128, 512], F32), "p1": ("psum", [128, 512], F32), "p2": ("psum", [128, 512], F32),
+    "p3a": ("psum", [128, 512], F32), "p3b": ("psum", [128, 512], F32), "p4": ("psum", [128, 512], F32), "p5": ("psum", [128, 512], F32),
+}
+SEMAPHORES = ["exin", "xin", "exa", "arr", "ls"] + ["e%d" % k for k in range(64)]
+WORLD = 256
+
+
+def plan(cores, topo):
+    n = len(cores)
+    lead, z = [], []
+    for r in range(n):
+        m = [q for q in range(r) if topo.mates(cores[r], cores[q])]
+        if m:
+            z.append(z[m[0]])
+        else:
+            z.append(len(lead))
+            lead.append(r)
+    out = []
+    for r in range(n):
+        mate = [d for d in range(n) if d != r and topo.mates(cores[r], cores[d])][0]
+        same, cross = {}, {}
+        for dl in range(1, len(lead)):
+            for d in range(n):
+                if z[d] == z[r] ^ dl:
+                    (same if topo.same_plane(cores[r], cores[d]) else cross)[dl] = d
+        mine, his = [cross[1], mate, same[2], same[3]], [cross[2], cross[3], same[1], r]
+        R = cores[r]
+        H = [c for c in range(WORLD) if c != R and topo.host(c) == topo.host(R) and topo.chip(c) == topo.chip(R)
+             and topo.die(c) != topo.die(R) and all(topo.may_write(c, cores[d]) for d in his)][0]
+        out.append((H, mine, his))
+    return out
+
+
+def rank_program(g, core, T, topo):
+    cores = list(T.cores)
+    pl = plan(cores, topo)
+    rank, helper = T.rank_of(core), False
+    if rank is None:
+        own = [r for r in range(len(cores)) if pl[r][0] == core]
+        if not own:
+            return
+        rank, helper = own[0], True
+    R, (H, mine, his) = cores[rank], pl[rank]
+    dests = his if helper else mine
+    v, s, t, sy = g.vector, g.scalar, g.tensor, g.sync
+    sem = T.sem
+
+    used, seen = [0], {}
+
+    def ev():
+        used[0] += 1
+        return [sem["e%d" % (used[0] - 1)], 0, used[0]]
+
+    def done(ins, e=None, n=1):
+        e = e or ev()
+        ins.then_inc(e[0], n)
+        e[1] += n
+        return e
+
+    def need(q, name, *es):
+        for e in es:
+            if (name, e[2]) not in seen:
+                seen[(name, e[2])] = 1
+                q.wait_ge(e[0], e[1])
+
+    def bits(m):
+        return bin(m).count("1")
+
+    far = [c for c in cores if topo.chip(c) != topo.chip(R) or topo.host(c) != topo.host(R)]
+    m_off = topo.mask(core, far[0])
+    m_on = topo.mask(core, R if helper else H)
+    n_ls = 0
+
+    if not helper:
+        d_ex = done(sy.dma_start(T.e16[0:16, :], T.ex[:]), None, 16)
+        d_exd = done(s.dma_start(T.exall[rank], T.ex[:]), None, 16)
+        d_x0 = done(sy.dma_start(T.xs[:, 0:1024], T.x[:, 0:1024]), None, 16)
+        d_x1 = done(s.dma_start(T.xs[:, 1024:2048], T.x[:, 1024:2048]), None, 16)
+
+    i_p = done(g.iota(T.pcol[:], [[0, 1]], 0, 1))
+    i_i = done(g.iota(T.rowi[:], [[0, 9], [1, 16]], 0, 0, allow_small_or_imprecise_dtypes=True))
+    i_g = done(g.iota(T.rowg[:], [[1, 8], [0, 16]], 0, 0, allow_small_or_imprecise_dtypes=True))
+    i_r = done(g.iota(T.row[:], [[1, 256]], 0, 0, allow_small_or_imprecise_dtypes=True))
+    if helper:
+        i_d = done(g.iota(T.dm[:], [[0, 8], [-8, 16]], 0, 1, allow_small_or_imprecise_dtypes=True))
+
+    if not helper:
+        need(g, "g", d_exd)
+        rid, pid = topo.addr(H, core)
+        to = DstId(rid=rid, pnc=pid)
+        m = m_on & m_off
+        g.remote_dma_fused([RemoteDMATransfer(dst_ids=[to, to], dma_engine_mask=m, remote_sem=sem.exin, srcs=[T.exall[rank]],
+                                              dsts=[T.e8[:], T.exall[rank]])], local_sem=sem.ls)
+        n_ls += bits(m)
+        for e, a in ((d_x0, 0), (d_x1, 1024)):
+            need(g, "g", e)
+            g.remote_dma(T.xs[:, a:a + 1024], T.xs[:, a:a + 1024], sem.xin, sem.ls, pid, rid, m_on)
+            n_ls += bits(m_on)
+        xe = [d_x0, d_x1]
+    else:
+        e_in = [sem.exin, 2 * bits(m_on & m_off), "exin"]
+        xe = [[sem.xin, 2 * bits(m_on), "xin"]]
+        need(g, "g", e_in)
+        ids, dsts = [], []
+        for d in range(len(cores)):
+            if d != rank:
+                rid, pid = topo.addr(cores[d], core)
+                ids.append(DstId(rid=rid, pnc=pid))
+                dsts.append(T.exall[rank])
+        g.remote_dma_fused([RemoteDMATransfer(dst_ids=ids, dma_engine_mask=m_off, remote_sem=sem.exa, srcs=[T.exall[rank]],
+                                              dsts=dsts)], local_sem=sem.ls)
+        n_ls += bits(m_off)
+
+    e_ka = ev()
+    for k in range(4):
+        done(v.memset(T.ka[32 * k:32 * k + 32, :], float(2 * dests[k])), e_ka)
+    e_sc0 = done(v.memset(T.sc[:, 0:1], 0.0))
+    e_z0 = done(v.memset(T.zw[:], 0.0))
+    done(v.memset(T.zk[:], 0.0), e_z0)
+    need(v, "v", i_p)
+    e_c = done(v.tensor_scalar(T.gi[:], T.pcol[:], 4, None, Op.arith_shift_right))
+    done(v.tensor_scalar(T.ii[:], T.pcol[:], 15, None, Op.bitwise_and), e_c)
+    done(v.tensor_scalar(T.kp[:], T.pcol[:], 4, 1, Op.arith_shift_right, Op.bitwise_and), e_c)
+    e_f = done(v.tensor_copy(T.pf[:], T.pcol[:]))
+    need(v, "v", e_c)
+    done(v.tensor_copy(T.gcol[:], T.gi[:]), e_f)
+    done(v.tensor_copy(T.icol[:], T.ii[:]), e_f)
+    done(v.tensor_copy(T.kpf[:], T.kp[:]), e_f)
+    need(v, "v", e_f, e_ka, i_i)
+    e_k = done(v.tensor_tensor(T.kcol[:], T.ka[:], T.kpf[:], Op.add))
+    e_r16 = done(v.tensor_scalar(T.r16[0:16, :], T.rowi[0:16, 0:128], T.icol[0:16, :], None, Op.is_equal))
+    if helper:
+        need(v, "v", i_d)
+        for h in range(8):
+            done(v.tensor_scalar(T.rh[:, 128 * h:128 * h + 128], T.dm[:], float(h), None, Op.is_equal), e_r16)
+    e_l = done(v.tensor_scalar(T.lneg[0:16, :], T.rowi[0:16, 0:128], -16.0, T.icol[0:16, :], Op.mult, Op.subtract))
+    done(v.tensor_scalar(T.lpos[0:16, :], T.rowi[0:16, 0:16], 16.0, T.icol[0:16, :], Op.mult, Op.add), e_l)
+    need(v, "v", i_g)
+    e_b = done(v.tensor_scalar(T.mb[:], T.rowg[:], T.gcol[:], None, Op.is_equal))
+    need(v, "v", i_r)
+    e_mg = done(v.tensor_scalar(T.mg[:], T.row[:, 0:128], T.pf[:], None, Op.is_gt))
+    need(v, "v", e_b, e_mg)
+    e_a = done(v.tensor_tensor(T.ma[:], T.mb[:], T.mg[:], Op.mult))
+    e_kw = done(v.tensor_scalar(T.kw[:], T.gcol[:], 256.0, 256.0, Op.mult, Op.add))
+    e_w = done(v.tensor_scalar(T.w0[:], T.icol[:], 0.0, None, Op.is_equal))
+    done(v.tensor_scalar(T.w1[:], T.icol[:], 1.0, None, Op.is_equal), e_w)
+    need(v, "v", e_z0, e_kw)
+    e_zw = done(v.tensor_scalar(T.zw[:, 112:128], T.rowi[:, 0:16], T.icol[:], None, Op.is_equal))
+    done(v.tensor_scalar(T.zk[:, 112:128], T.rowi[:, 0:16], T.icol[:], T.kw[:], Op.is_equal, Op.mult), e_zw)
+    e_win = done(v.memset(T.win[:, 256:1280], 0.0))
+
+    need(s, "s", i_r)
+    for k in range(4):
+        done(s.activation(T.win[:, 1280 + 256 * k:1536 + 256 * k], T.row[:], Fn.Copy, scale=0.0), e_win)
+    need(s, "s", e_w)
+    e_vals = done(s.activation(T.vals[:], T.row[:], Fn.Identity, bias=T.w1[:], scale=T.w0[:]))
+
+    need(t, "t", e_r16, e_l)
+    t.matmul(T.p1[:, 0:128], T.r16[0:16, :], T.lneg[0:16, :], True, False)
+    t.matmul(T.p2[:, 0:16], T.r16[0:16, :], T.lpos[0:16, :], True, False)
+
+    if helper:
+        need(v, "v", e_in)
+        e_eb = done(v.tensor_copy(T.e8b[:], T.e8[:]))
+        need(t, "t", e_eb)
+        for h in range(8):
+            ins = t.matmul(T.pb[:, 16 * h:16 * h + 16], T.rh[:, 128 * h:128 * h + 128], T.e8b[:], True, True)
+    else:
+        need(v, "v", d_ex)
+        e_eb = done(v.tensor_copy(T.e16b[0:16, :], T.e16[0:16, :]))
+        need(t, "t", e_eb)
+        ins = t.matmul(T.pb[:, 0:128], T.r16[0:16, :], T.e16b[0:16, :], True, True)
+    e_pb = done(ins)
+    need(v, "v", e_w)
+    e_wg = done(v.tensor_scalar(T.wg[:], T.gcol[:], T.w1[:], 256.0, Op.mult, Op.mult))
+    need(v, "v", e_pb, e_k)
+    e_oh = done(v.tensor_scalar(T.oh[:], T.pb[:, 0:128], T.kcol[:], None, Op.is_equal))
+    need(v, "v", e_oh, e_sc0)
+    e_sc = done(v.tensor_tensor_scan(T.sc[:, 1:129], T.oh[:], T.oh[:], 0.0, Op.add, Op.max))
+    need(v, "v", e_wg)
+    e_ww = done(v.tensor_tensor(T.ww[:], T.w0[:], T.wg[:], Op.add))
+    need(t, "t", e_a, e_b, e_oh)
+    t.matmul(T.p1[:, 0:128], T.ma[:], T.oh[:], False, False)
+    need(t, "t", e_sc0, e_sc)
+    e_p1 = done(t.matmul(T.p1[:, 0:128], T.mb[:], T.sc[:, 0:128], False, True))
+    need(t, "t", e_zw)
+    for k in range(8):
+        t.matmul(T.p2[:, 0:16], T.zk[:, 112 - 16 * k:240 - 16 * k], T.oh[:, 16 * k:16 * k + 16], False, False)
+    need(v, "v", e_p1)
+    e_pr = done(v.tensor_tensor(T.pr[:], T.p1[:, 0:128], T.oh[:], Op.mult))
+    need(v, "v", e_ww)
+    e_zl = done(v.tensor_scalar(T.zl[:, 0:143], T.rowi[:, 0:143], 15.0, T.ww[:], Op.is_equal, Op.mult))
+    need(t, "t", e_pr)
+    for k in range(8):
+        ins = t.matmul(T.p2[:, 0:16], T.zw[:, 112 - 16 * k:240 - 16 * k], T.pr[:, 16 * k:16 * k + 16], False, k == 7)
+    e_p2 = done(ins)
+    need(v, "v", e_p2)
+    e_of = done(v.tensor_copy(T.offs[:], T.p2[:, 0:16]))
+    need(v, "v", e_of, e_win, e_vals)
+    e_sct = done(v.tensor_copy(T.win[:, 0:2304].indirect(T.offs[:, 0:16]), T.vals[:]))
+    need(t, "t", e_zl, e_win, e_sct)
+    e_p3 = []
+    for b, P in ((0, T.p3a), (1, T.p3b)):
+        for lo in range(16):
+            a = 256 + 1024 * b + lo
+            ins = t.matmul(P[:, 0:64], T.zl[:, 15 - lo:143 - lo], T.win[:, a:a + 1009:16], lo == 0, lo == 15)
+        e_p3.append(done(ins))
+
+    e_ox, e_gv, e_gs = [], [], []
+
+    def conv(b):
+        need(v, "v", e_p3[b])
+        e_ox.append(done(v.tensor_copy(T.offx[:, 64 * b:64 * b + 64], (T.p3a, T.p3b)[b][:, 0:64])))
+
+    conv(0)
+    for k in range(4):
+        if k == 1:
+            conv(1)
+        need(v, "v", e_ox[k // 2], *xe)
+        c, o = 512 * k, 32 * k
+        e_gv.append(done(v.tensor_copy(T.sb[:, c:c + 256], T.xs[:, 0:2048].indirect(T.offx[:, o:o + 16]))))
+        need(s, "s", e_ox[k // 2], *xe)
+        e_gs.append(done(s.activation(T.sb[:, c + 256:c + 512], T.xs[:, 0:2048].indirect(T.offx[:, o + 16:o + 32]), Fn.Copy)))
+        need(g, "g", e_gv[k], e_gs[k])
+        d = cores[dests[k]]
+        rid, pid = topo.addr(d, core)
+        m = m_on & ~m_off if d == R else topo.mask(core, d)
+        g.remote_dma(T.land[:, 512 * rank:512 * rank + 512], T.sb[:, c:c + 512], sem.arr, sem.ls, pid, rid, m)
+        n_ls += bits(m)
+
+    if not helper:
+        e_rc = done(v.memset(T.land[:, 4096:4112], 0.0))
+        done(v.tensor_scalar(T.rbs[:], T.rowg[:], T.gcol[:], None, Op.is_ge), e_rc)
+        done(v.tensor_scalar(T.rb[:], T.rowg[:], T.gcol[:], None, Op.is_equal), e_rc)
+        done(v.tensor_scalar(T.rd[:], T.rowi[:, 0:128], T.icol[:], None, Op.is_equal), e_rc)
+        e_pl = done(v.tensor_scalar(T.pl[:], T.row[:, 0:60], 16.0, T.icol[:], Op.mult, Op.add))
+        need(v, "v", e_pl)
+        done(v.tensor_copy(T.pc[0:16, 0:60], T.pl[0:16, :]), e_rc)
+        done(v.tensor_scalar(T.pc[0:16, 60:120], T.pl[0:16, :], 256.0, None, Op.add), e_rc)
+        need(sy, "y", d_exd, [sem.exa, (len(cores) - 1) * bits(m_off), "exa"])
+        d_all = done(sy.dma_start(T.allex[:], T.exall[:]), None, 16)
+        need(v, "v", d_all)
+        e_q = ev()
+        for e, q in ((0, T.eq0), (1, T.eq1)):
+            done(v.tensor_scalar(q[:], T.allex[:], float(2 * rank + e), None, Op.is_equal), e_q)
+        need(v, "v", e_q)
+        e_cnt = ev()
+        for e, q in ((0, T.eq0), (1, T.eq1)):
+            done(v.tensor_reduce(T.cnt[:, e:e + 1], q[:], AxisListType.X, Op.add), e_cnt)
+        need(t, "t", e_rc)
+        t.matmul(T.p5[:, 0:120], T.rd[0:16, :], T.pc[0:16, :], True, False)
+        need(t, "t", e_cnt)
+        t.matmul(T.p4[:, 0:2], T.rbs[:], T.cnt[:], True, True)
+        e_p4 = done(t.matmul(T.p4[:, 2:4], T.rb[:], T.cnt[:], True, True))
+        need(v, "v", e_p4)
+        e_wc = done(v.tensor_scalar(T.wc[:], T.p4[:, 2:4], -1.0, 512.0, Op.mult, Op.add))
+        need(v, "v", e_wc)
+        e_u = ev()
+        for e in range(2):
+            done(v.tensor_scalar(T.uu[:, 60 * e:60 * e + 60], T.pl[:], T.p4[:, e:e + 1], T.wc[:, e:e + 1], Op.is_ge, Op.mult), e_u)
+        need(t, "t", e_u)
+        e_p5 = done(t.matmul(T.p5[:, 0:120], T.rd[:], T.uu[:], False, True))
+        need(v, "v", e_p5)
+        e_ro = done(v.tensor_scalar(T.roff[:], T.p5[:, 0:120], 4096.0, None, Op.min))
+        arrived = [sem.arr, len(mine) * bits(m_off) + (len(his) - 1) * bits(m_off) + bits(m_on & ~m_off), "arr"]
+        d_y, d_z = ev(), ev()
+        for h in range(2):
+            a, o = 480 * h, 30 * h
+            need(v, "v", e_ro, e_rc, arrived)
+            ea = done(v.tensor_copy(T.yt[:, a:a + 480], T.land[:, 0:4112].indirect(T.roff[:, o:o + 30])))
+            need(s, "s", e_ro, e_rc, arrived)
+            eb = done(s.activation(T.yt[:, 960 + a:1440 + a], T.land[:, 0:4112].indirect(T.roff[:, 60 + o:90 + o]), Fn.Copy))
+            need(sy, "y", ea)
+            done(sy.dma_start(T.y[:, a:a + 480], T.yt[:, a:a + 480]), d_y, 16)
+            q, nm, dd = (sy, "y", d_y) if h == 0 else (s, "s", d_z)
+            need(q, nm, eb)
+            done(q.dma_start(T.y[:, 960 + a:1440 + a], T.yt[:, 960 + a:1440 + a]), dd, 16)
+        need(sy, "y", d_y)
+        need(s, "s", d_z)
+    g.wait_ge(sem.ls, n_ls)

@@ -1,33 +1,32 @@
 from concourse.bass import DstId, RemoteDMATransfer
 from concourse.mybir import AluOpType as Op, AxisListType, ActivationFunctionType as Fn
 
+PIECES = 3
 BF, F32, I32, U16 = "bfloat16", "float32", "int32", "uint16"
 SCRATCH = {
     "exall": ("dram", [8, 128, 16], I32),
     "e16": ("sbuf", [128, 128], I32), "e16b": ("sbuf", [128, 128], BF),
-    "e8": ("sbuf", [128, 16], I32), "e8b": ("sbuf", [128, 16], BF),
     "xs": ("sbuf", [128, 2048], BF), "sb": ("sbuf", [128, 2048], BF),
     "land": ("sbuf", [128, 4112], BF), "yt": ("sbuf", [128, 1920], BF),
-    "pcol": ("sbuf", [128, 1], I32), "gi": ("sbuf", [128, 1], I32), "ii": ("sbuf", [128, 1], I32), "kp": ("sbuf", [128, 1], I32),
-    "gcol": ("sbuf", [128, 1], F32), "icol": ("sbuf", [128, 1], F32), "pf": ("sbuf", [128, 1], F32), "kpf": ("sbuf", [128, 1], F32),
-    "ka": ("sbuf", [128, 1], F32), "kcol": ("sbuf", [128, 1], F32), "kw": ("sbuf", [128, 1], F32),
-    "w0": ("sbuf", [128, 1], F32), "w1": ("sbuf", [128, 1], F32), "wg": ("sbuf", [128, 1], F32), "ww": ("sbuf", [128, 1], F32),
+    "ci": ("sbuf", [128, 8], I32), "cf": ("sbuf", [128, 16], F32),
+    "ka": ("sbuf", [128, 2], F32), "kcol": ("sbuf", [128, 2], F32),
     "rowi": ("sbuf", [128, 144], BF), "rowg": ("sbuf", [128, 128], BF), "row": ("sbuf", [128, 256], BF),
-    "r16": ("sbuf", [128, 128], BF), "lneg": ("sbuf", [128, 128], BF), "lpos": ("sbuf", [128, 16], BF),
-    "mb": ("sbuf", [128, 128], BF), "mg": ("sbuf", [128, 128], BF), "ma": ("sbuf", [128, 128], BF),
+    "r16": ("sbuf", [128, 128], BF), "lneg": ("sbuf", [128, 128], BF), "lpos": ("sbuf", [128, 128], BF),
+    "mb": ("sbuf", [128, 128], BF), "mg": ("sbuf", [128, 128], BF), "mn": ("sbuf", [128, 128], BF), "mbs": ("sbuf", [128, 128], BF),
     "zw": ("sbuf", [128, 240], BF), "zk": ("sbuf", [128, 240], BF), "zl": ("sbuf", [128, 144], BF),
-    "dm": ("sbuf", [128, 128], BF), "rh": ("sbuf", [128, 1024], BF),
-    "oh": ("sbuf", [128, 128], BF), "sc": ("sbuf", [128, 136], BF), "pr": ("sbuf", [128, 128], BF),
-    "offs": ("sbuf", [128, 16], U16), "vals": ("sbuf", [128, 256], BF), "win": ("sbuf", [128, 2304], BF),
+    "oh0": ("sbuf", [128, 128], BF), "pr0": ("sbuf", [128, 128], BF),
+    "oh1": ("sbuf", [128, 128], BF), "pr1": ("sbuf", [128, 128], BF), "sc": ("sbuf", [128, 272], BF),
+    "offs0": ("sbuf", [128, 16], U16), "offs1": ("sbuf", [128, 16], U16),
+    "vals": ("sbuf", [128, 256], BF), "win": ("sbuf", [128, 2304], BF),
     "offx": ("sbuf", [128, 128], U16),
     "allex": ("sbuf", [128, 128], I32), "eq0": ("sbuf", [128, 128], F32), "eq1": ("sbuf", [128, 128], F32),
-    "cnt": ("sbuf", [128, 2], F32), "rbs": ("sbuf", [128, 128], F32), "rb": ("sbuf", [128, 128], F32), "rd": ("sbuf", [128, 128], F32),
-    "pl": ("sbuf", [128, 60], F32), "pc": ("sbuf", [128, 120], F32), "wc": ("sbuf", [128, 2], F32), "uu": ("sbuf", [128, 120], F32),
-    "roff": ("sbuf", [128, 120], U16),
-    "pb": ("psum", [128, 512], F32), "p1": ("psum", [128, 512], F32), "p2": ("psum", [128, 512], F32),
-    "p3a": ("psum", [128, 512], F32), "p3b": ("psum", [128, 512], F32), "p4": ("psum", [128, 512], F32), "p5": ("psum", [128, 512], F32),
+    "cnt": ("sbuf", [128, 2], F32), "cntb": ("sbuf", [128, 2], BF), "rc": ("sbuf", [128, 308], F32),
+    "wc": ("sbuf", [128, 2], F32), "uu": ("sbuf", [128, 120], F32), "roff": ("sbuf", [128, 120], U16),
+    "pb": ("psum", [128, 512], F32), "p10": ("psum", [128, 512], F32), "p11": ("psum", [128, 512], F32),
+    "p20": ("psum", [128, 512], F32), "p21": ("psum", [128, 512], F32),
+    "p3a": ("psum", [128, 512], F32), "p3b": ("psum", [128, 512], F32), "p5": ("psum", [128, 512], F32),
 }
-SEMAPHORES = ["exin", "xin", "exa", "arr", "ls"] + ["e%d" % k for k in range(64)]
+SEMAPHORES = ["cin", "xin", "oin", "exa", "arr", "ls"] + ["e%d" % k for k in range(80)]
 WORLD = 256
 
 
@@ -49,7 +48,7 @@ def plan(cores, topo):
             for d in range(n):
                 if z[d] == z[r] ^ dl:
                     (same if topo.same_plane(cores[r], cores[d]) else cross)[dl] = d
-        mine, his = [cross[1], mate, same[2], same[3]], [cross[2], cross[3], same[1], r]
+        mine, his = [cross[1], same[2], same[3], mate], [cross[2], cross[3], same[1], r]
         R = cores[r]
         H = [c for c in range(WORLD) if c != R and topo.host(c) == topo.host(R) and topo.chip(c) == topo.chip(R)
              and topo.die(c) != topo.die(R) and all(topo.may_write(c, cores[d]) for d in his)][0]
@@ -70,6 +69,10 @@ def rank_program(g, core, T, topo):
     dests = his if helper else mine
     v, s, t, sy = g.vector, g.scalar, g.tensor, g.sync
     sem = T.sem
+    pcol, gi, ii, kp = [T.ci[:, k:k + 1] for k in range(4)]
+    gcol, icol, pf, kpf, kw, w0, w1, wg, ww = [T.cf[:, k:k + 1] for k in range(9)]
+    icol16 = T.cf[0:16, 1:2]
+    rd, plc = T.rc[:, 0:128], T.rc[:, 128:188]
 
     used, seen = [0], {}
 
@@ -103,128 +106,152 @@ def rank_program(g, core, T, topo):
         d_x0 = done(sy.dma_start(T.xs[:, 0:1024], T.x[:, 0:1024]), None, 16)
         d_x1 = done(s.dma_start(T.xs[:, 1024:2048], T.x[:, 1024:2048]), None, 16)
 
-    i_p = done(g.iota(T.pcol[:], [[0, 1]], 0, 1))
+    i_p = done(g.iota(pcol, [[0, 1]], 0, 1))
     i_i = done(g.iota(T.rowi[:], [[0, 9], [1, 16]], 0, 0, allow_small_or_imprecise_dtypes=True))
-    i_g = done(g.iota(T.rowg[:], [[1, 8], [0, 16]], 0, 0, allow_small_or_imprecise_dtypes=True))
+    if not helper:
+        i_g = done(g.iota(T.rowg[:], [[1, 8], [0, 16]], 0, 0, allow_small_or_imprecise_dtypes=True))
     i_r = done(g.iota(T.row[:], [[1, 256]], 0, 0, allow_small_or_imprecise_dtypes=True))
-    if helper:
-        i_d = done(g.iota(T.dm[:], [[0, 8], [-8, 16]], 0, 1, allow_small_or_imprecise_dtypes=True))
 
     if not helper:
+        rid_h, pid_h = topo.addr(H, core)
         need(g, "g", d_exd)
-        rid, pid = topo.addr(H, core)
-        to = DstId(rid=rid, pnc=pid)
-        m = m_on & m_off
-        g.remote_dma_fused([RemoteDMATransfer(dst_ids=[to, to], dma_engine_mask=m, remote_sem=sem.exin, srcs=[T.exall[rank]],
-                                              dsts=[T.e8[:], T.exall[rank]])], local_sem=sem.ls)
-        n_ls += bits(m)
-        for e, a in ((d_x0, 0), (d_x1, 1024)):
-            need(g, "g", e)
-            g.remote_dma(T.xs[:, a:a + 1024], T.xs[:, a:a + 1024], sem.xin, sem.ls, pid, rid, m_on)
-            n_ls += bits(m_on)
-        xe = [d_x0, d_x1]
-    else:
-        e_in = [sem.exin, 2 * bits(m_on & m_off), "exin"]
-        xe = [[sem.xin, 2 * bits(m_on), "xin"]]
-        need(g, "g", e_in)
-        ids, dsts = [], []
+        ids = []
         for d in range(len(cores)):
             if d != rank:
                 rid, pid = topo.addr(cores[d], core)
                 ids.append(DstId(rid=rid, pnc=pid))
-                dsts.append(T.exall[rank])
         g.remote_dma_fused([RemoteDMATransfer(dst_ids=ids, dma_engine_mask=m_off, remote_sem=sem.exa, srcs=[T.exall[rank]],
-                                              dsts=dsts)], local_sem=sem.ls)
-        n_ls += bits(m_off)
+                                              dsts=[T.exall[rank] for d in ids])], local_sem=sem.ls)
+        need(g, "g", d_x0)
+        g.remote_dma(T.xs[:, 0:1024], T.xs[:, 0:1024], sem.xin, sem.ls, pid_h, rid_h, m_on)
+        n_ls += bits(m_off) + bits(m_on)
+        xe = [d_x0, d_x1]
+    else:
+        xe = [[sem.xin, 2 * bits(m_on), "xin"]]
 
-    e_ka = ev()
-    for k in range(4):
-        done(v.memset(T.ka[32 * k:32 * k + 32, :], float(2 * dests[k])), e_ka)
-    e_sc0 = done(v.memset(T.sc[:, 0:1], 0.0))
-    e_z0 = done(v.memset(T.zw[:], 0.0))
-    done(v.memset(T.zk[:], 0.0), e_z0)
+    if not helper:
+        e_ka = ev()
+        for i, ds in ((0, his), (1, mine)):
+            for k in range(4):
+                done(v.memset(T.ka[32 * k:32 * k + 32, i:i + 1], float(2 * ds[k])), e_ka)
+        e_sz = done(v.memset(T.sc[:, 0:137:136], 0.0))
+        e_z0 = done(v.memset(T.zw[:], 0.0))
+        done(v.memset(T.zk[:], 0.0), e_z0)
     need(v, "v", i_p)
-    e_c = done(v.tensor_scalar(T.gi[:], T.pcol[:], 4, None, Op.arith_shift_right))
-    done(v.tensor_scalar(T.ii[:], T.pcol[:], 15, None, Op.bitwise_and), e_c)
-    done(v.tensor_scalar(T.kp[:], T.pcol[:], 4, 1, Op.arith_shift_right, Op.bitwise_and), e_c)
-    e_f = done(v.tensor_copy(T.pf[:], T.pcol[:]))
+    e_c = done(v.tensor_scalar(gi, pcol, 4, None, Op.arith_shift_right))
+    done(v.tensor_scalar(ii, pcol, 15, None, Op.bitwise_and), e_c)
+    if not helper:
+        done(v.tensor_scalar(kp, pcol, 4, 1, Op.arith_shift_right, Op.bitwise_and), e_c)
+        e_f2 = done(v.tensor_copy(pf, pcol))
     need(v, "v", e_c)
-    done(v.tensor_copy(T.gcol[:], T.gi[:]), e_f)
-    done(v.tensor_copy(T.icol[:], T.ii[:]), e_f)
-    done(v.tensor_copy(T.kpf[:], T.kp[:]), e_f)
-    need(v, "v", e_f, e_ka, i_i)
-    e_k = done(v.tensor_tensor(T.kcol[:], T.ka[:], T.kpf[:], Op.add))
-    e_r16 = done(v.tensor_scalar(T.r16[0:16, :], T.rowi[0:16, 0:128], T.icol[0:16, :], None, Op.is_equal))
-    if helper:
-        need(v, "v", i_d)
-        for h in range(8):
-            done(v.tensor_scalar(T.rh[:, 128 * h:128 * h + 128], T.dm[:], float(h), None, Op.is_equal), e_r16)
-    e_l = done(v.tensor_scalar(T.lneg[0:16, :], T.rowi[0:16, 0:128], -16.0, T.icol[0:16, :], Op.mult, Op.subtract))
-    done(v.tensor_scalar(T.lpos[0:16, :], T.rowi[0:16, 0:16], 16.0, T.icol[0:16, :], Op.mult, Op.add), e_l)
-    need(v, "v", i_g)
-    e_b = done(v.tensor_scalar(T.mb[:], T.rowg[:], T.gcol[:], None, Op.is_equal))
-    need(v, "v", i_r)
-    e_mg = done(v.tensor_scalar(T.mg[:], T.row[:, 0:128], T.pf[:], None, Op.is_gt))
-    need(v, "v", e_b, e_mg)
-    e_a = done(v.tensor_tensor(T.ma[:], T.mb[:], T.mg[:], Op.mult))
-    e_kw = done(v.tensor_scalar(T.kw[:], T.gcol[:], 256.0, 256.0, Op.mult, Op.add))
-    e_w = done(v.tensor_scalar(T.w0[:], T.icol[:], 0.0, None, Op.is_equal))
-    done(v.tensor_scalar(T.w1[:], T.icol[:], 1.0, None, Op.is_equal), e_w)
-    need(v, "v", e_z0, e_kw)
-    e_zw = done(v.tensor_scalar(T.zw[:, 112:128], T.rowi[:, 0:16], T.icol[:], None, Op.is_equal))
-    done(v.tensor_scalar(T.zk[:, 112:128], T.rowi[:, 0:16], T.icol[:], T.kw[:], Op.is_equal, Op.mult), e_zw)
-    e_win = done(v.memset(T.win[:, 256:1280], 0.0))
+    e_f = done(v.tensor_copy(icol, ii))
+    done(v.tensor_copy(gcol, gi), e_f)
+    if not helper:
+        done(v.tensor_copy(kpf, kp), e_f2)
+    need(v, "v", e_f, i_i)
 
+    def col_weights():
+        e = done(v.tensor_scalar(w0, icol, 0.0, None, Op.is_equal))
+        return done(v.tensor_scalar(w1, icol, 1.0, None, Op.is_equal), e)
+
+    def fold_matrix():
+        need(v, "v", e_w)
+        e_wg = done(v.tensor_scalar(wg, gcol, w1, 256.0, Op.mult, Op.mult))
+        need(v, "v", e_wg)
+        e_ww = done(v.tensor_tensor(ww, w0, wg, Op.add))
+        need(v, "v", e_ww)
+        return done(v.tensor_scalar(T.zl[:, 0:143], T.rowi[:, 0:143], 15.0, ww, Op.is_equal, Op.mult))
+
+    e_win, e_win2 = ev(), ev()
+    e_cin = [sem.cin, bits(m_on), "cin"]
+    if helper:
+        need(v, "v", i_r)
+        e_rc = done(v.tensor_scalar(plc, T.row[:, 0:60], 16.0, icol, Op.mult, Op.add))
+        need(v, "v", e_rc)
+        done(v.tensor_scalar(rd, T.rowi[:, 0:128], icol, None, Op.is_equal), e_rc)
+        done(v.tensor_copy(T.rc[:, 188:248], plc), e_rc)
+        done(v.tensor_scalar(T.rc[:, 248:308], plc, 256.0, None, Op.add), e_rc)
+        need(g, "g", e_rc)
+        rid, pid = topo.addr(R, core)
+        g.remote_dma(T.rc[:], T.rc[:], sem.cin, sem.ls, pid, rid, m_on)
+        n_ls += bits(m_on)
+        e_w = col_weights()
+        e_zl = fold_matrix()
+        done(v.memset(T.win[:, 256:1280], 0.0), e_win)
+        offs, e_of = T.offs0, [sem.oin, bits(m_on), "oin"]
+    else:
+        e_r16 = done(v.tensor_scalar(T.r16[0:16, :], T.rowi[0:16, 0:128], icol16, None, Op.is_equal))
+        need(v, "v", e_ka, e_f2)
+        e_k = done(v.tensor_scalar(T.kcol[:], T.ka[:], kpf, None, Op.add))
+        need(v, "v", i_g)
+        e_b = done(v.tensor_scalar(T.mb[:], T.rowg[:], gcol, None, Op.is_equal))
+        done(v.tensor_scalar(T.mn[:], T.rowg[:], gcol, -1.0, Op.is_gt, Op.mult), e_b)
+        need(v, "v", i_r)
+        done(v.tensor_scalar(T.mg[:], T.row[:, 0:128], pf, None, Op.is_gt), e_b)
+        need(s, "s", e_f, i_i)
+        e_lp = done(s.activation(T.lpos[0:16, :], T.rowi[0:16, 0:128], Fn.Identity, bias=icol16, scale=16.0))
+        need(s, "s", e_lp)
+        e_l = done(s.activation(T.lneg[0:16, :], T.lpos[0:16, :], Fn.Copy, scale=-1.0))
     need(s, "s", i_r)
     for k in range(4):
-        done(s.activation(T.win[:, 1280 + 256 * k:1536 + 256 * k], T.row[:], Fn.Copy, scale=0.0), e_win)
-    need(s, "s", e_w)
-    e_vals = done(s.activation(T.vals[:], T.row[:], Fn.Identity, bias=T.w1[:], scale=T.w0[:]))
+        done(s.activation(T.win[:, 1280 + 256 * k:1536 + 256 * k], T.row[:], Fn.Copy, scale=0.0), e_win2)
 
-    need(t, "t", e_r16, e_l)
-    t.matmul(T.p1[:, 0:128], T.r16[0:16, :], T.lneg[0:16, :], True, False)
-    t.matmul(T.p2[:, 0:16], T.r16[0:16, :], T.lpos[0:16, :], True, False)
-
-    if helper:
-        need(v, "v", e_in)
-        e_eb = done(v.tensor_copy(T.e8b[:], T.e8[:]))
-        need(t, "t", e_eb)
-        for h in range(8):
-            ins = t.matmul(T.pb[:, 16 * h:16 * h + 16], T.rh[:, 128 * h:128 * h + 128], T.e8b[:], True, True)
-    else:
+    if not helper:
+        oh, pr, p1, p2, offs2 = (T.oh0, T.oh1), (T.pr0, T.pr1), (T.p10, T.p11), (T.p20, T.p21), (T.offs0, T.offs1)
+        need(t, "t", e_r16, e_lp, e_l)
+        for i in range(2):
+            t.matmul(p1[i][:, 0:128], T.r16[0:16, :], T.lneg[0:16, :], True, False)
+            t.matmul(p2[i][:, 0:16], T.r16[0:16, :], T.lpos[0:16, 0:16], True, False)
         need(v, "v", d_ex)
         e_eb = done(v.tensor_copy(T.e16b[0:16, :], T.e16[0:16, :]))
         need(t, "t", e_eb)
-        ins = t.matmul(T.pb[:, 0:128], T.r16[0:16, :], T.e16b[0:16, :], True, True)
-    e_pb = done(ins)
-    need(v, "v", e_w)
-    e_wg = done(v.tensor_scalar(T.wg[:], T.gcol[:], T.w1[:], 256.0, Op.mult, Op.mult))
-    need(v, "v", e_pb, e_k)
-    e_oh = done(v.tensor_scalar(T.oh[:], T.pb[:, 0:128], T.kcol[:], None, Op.is_equal))
-    need(v, "v", e_oh, e_sc0)
-    e_sc = done(v.tensor_tensor_scan(T.sc[:, 1:129], T.oh[:], T.oh[:], 0.0, Op.add, Op.max))
-    need(v, "v", e_wg)
-    e_ww = done(v.tensor_tensor(T.ww[:], T.w0[:], T.wg[:], Op.add))
-    need(t, "t", e_a, e_b, e_oh)
-    t.matmul(T.p1[:, 0:128], T.ma[:], T.oh[:], False, False)
-    need(t, "t", e_sc0, e_sc)
-    e_p1 = done(t.matmul(T.p1[:, 0:128], T.mb[:], T.sc[:, 0:128], False, True))
-    need(t, "t", e_zw)
-    for k in range(8):
-        t.matmul(T.p2[:, 0:16], T.zk[:, 112 - 16 * k:240 - 16 * k], T.oh[:, 16 * k:16 * k + 16], False, False)
-    need(v, "v", e_p1)
-    e_pr = done(v.tensor_tensor(T.pr[:], T.p1[:, 0:128], T.oh[:], Op.mult))
-    need(v, "v", e_ww)
-    e_zl = done(v.tensor_scalar(T.zl[:, 0:143], T.rowi[:, 0:143], 15.0, T.ww[:], Op.is_equal, Op.mult))
-    need(t, "t", e_pr)
-    for k in range(8):
-        ins = t.matmul(T.p2[:, 0:16], T.zw[:, 112 - 16 * k:240 - 16 * k], T.pr[:, 16 * k:16 * k + 16], False, k == 7)
-    e_p2 = done(ins)
-    need(v, "v", e_p2)
-    e_of = done(v.tensor_copy(T.offs[:], T.p2[:, 0:16]))
-    need(v, "v", e_of, e_win, e_vals)
-    e_sct = done(v.tensor_copy(T.win[:, 0:2304].indirect(T.offs[:, 0:16]), T.vals[:]))
-    need(t, "t", e_zl, e_win, e_sct)
+        e_pb = done(t.matmul(T.pb[:, 0:128], T.r16[0:16, :], T.e16b[0:16, :], True, True))
+        e_w = col_weights()
+        e_kw = done(v.tensor_scalar(kw, gcol, 256.0, 256.0, Op.mult, Op.add))
+        need(v, "v", e_pb, e_k)
+        e_oh, e_sc = [], []
+        for i in range(2):
+            e_oh.append(done(v.tensor_scalar(oh[i][:], T.pb[:, 0:128], T.kcol[:, i:i + 1], None, Op.is_equal)))
+            need(v, "v", e_oh[i], e_sz)
+            e_sc.append(done(v.tensor_tensor_scan(T.sc[:, 136 * i + 1:136 * i + 129], oh[i][:], oh[i][:], 0.0, Op.add, Op.max)))
+            if i == 0:
+                need(v, "v", e_z0, e_kw)
+                e_zk = done(v.tensor_scalar(T.zk[:, 112:128], T.rowi[:, 0:16], icol, kw, Op.is_equal, Op.mult))
+                e_zw = done(v.tensor_scalar(T.zw[:, 112:128], T.rowi[:, 0:16], icol, None, Op.is_equal))
+        for i in range(2):
+            need(t, "t", e_b, e_oh[i])
+            t.matmul(p1[i][:, 0:128], T.mg[:], oh[i][:], False, False)
+            t.matmul(p1[i][:, 0:128], T.mn[:], oh[i][:], False, False)
+            need(t, "t", e_sz, e_sc[i])
+            e_p1 = done(t.matmul(p1[i][:, 0:128], T.mb[:], T.sc[:, 136 * i:136 * i + 128], False, True))
+            need(t, "t", e_zk)
+            for k in range(8):
+                t.matmul(p2[i][:, 0:16], T.zk[:, 112 - 16 * k:240 - 16 * k], oh[i][:, 16 * k:16 * k + 16], False, False)
+            need(v, "v", e_p1)
+            e_pr = done(v.tensor_tensor(pr[i][:], p1[i][:, 0:128], oh[i][:], Op.mult))
+            if i == 0:
+                e_zl = fold_matrix()
+            else:
+                done(v.memset(T.win[:, 256:1280], 0.0), e_win)
+            need(t, "t", e_zw, e_pr)
+            for k in range(8):
+                ins = t.matmul(p2[i][:, 0:16], T.zw[:, 112 - 16 * k:240 - 16 * k], pr[i][:, 16 * k:16 * k + 16], False, k == 7)
+            e_p2 = done(ins)
+            need(v, "v", e_p2)
+            e_of = done(v.tensor_copy(offs2[i][:], p2[i][:, 0:16]))
+            if i == 0:
+                need(g, "g", e_of)
+                g.remote_dma(T.offs0[:], T.offs0[:], sem.oin, sem.ls, pid_h, rid_h, m_on)
+                need(g, "g", d_x1)
+                g.remote_dma(T.xs[:, 1024:2048], T.xs[:, 1024:2048], sem.xin, sem.ls, pid_h, rid_h, m_on)
+                n_ls += 2 * bits(m_on)
+        offs = T.offs1
+
+    need(s, "s", e_w)
+    e_vals = done(s.activation(T.vals[:], T.row[:], Fn.Identity, bias=w1, scale=w0))
+    need(v, "v", e_of, e_win, e_win2, e_vals)
+    e_sct = done(v.tensor_copy(T.win[:, 0:2304].indirect(offs[:, 0:16]), T.vals[:]))
+    need(t, "t", e_zl, e_win, e_win2, e_sct)
     e_p3 = []
     for b, P in ((0, T.p3a), (1, T.p3b)):
         for lo in range(16):
@@ -232,7 +259,7 @@ def rank_program(g, core, T, topo):
             ins = t.matmul(P[:, 0:64], T.zl[:, 15 - lo:143 - lo], T.win[:, a:a + 1009:16], lo == 0, lo == 15)
         e_p3.append(done(ins))
 
-    e_ox, e_gv, e_gs = [], [], []
+    e_ox, e_gv, e_gs, e_q = [], [], [], ev()
 
     def conv(b):
         need(v, "v", e_p3[b])
@@ -240,7 +267,13 @@ def rank_program(g, core, T, topo):
 
     conv(0)
     for k in range(4):
-        if k == 1:
+        if k == 2:
+            if not helper:
+                need(sy, "y", d_exd, [sem.exa, (len(cores) - 1) * bits(m_off), "exa"])
+                d_all = done(sy.dma_start(T.allex[:], T.exall[:]), None, 16)
+                need(v, "v", d_all)
+                for e, q in ((0, T.eq0), (1, T.eq1)):
+                    done(v.tensor_scalar(q[:], T.allex[:], float(2 * rank + e), None, Op.is_equal), e_q)
             conv(1)
         need(v, "v", e_ox[k // 2], *xe)
         c, o = 512 * k, 32 * k
@@ -256,51 +289,42 @@ def rank_program(g, core, T, topo):
 
     if not helper:
         e_rc = done(v.memset(T.land[:, 4096:4112], 0.0))
-        done(v.tensor_scalar(T.rbs[:], T.rowg[:], T.gcol[:], None, Op.is_ge), e_rc)
-        done(v.tensor_scalar(T.rb[:], T.rowg[:], T.gcol[:], None, Op.is_equal), e_rc)
-        done(v.tensor_scalar(T.rd[:], T.rowi[:, 0:128], T.icol[:], None, Op.is_equal), e_rc)
-        e_pl = done(v.tensor_scalar(T.pl[:], T.row[:, 0:60], 16.0, T.icol[:], Op.mult, Op.add))
-        need(v, "v", e_pl)
-        done(v.tensor_copy(T.pc[0:16, 0:60], T.pl[0:16, :]), e_rc)
-        done(v.tensor_scalar(T.pc[0:16, 60:120], T.pl[0:16, :], 256.0, None, Op.add), e_rc)
-        need(sy, "y", d_exd, [sem.exa, (len(cores) - 1) * bits(m_off), "exa"])
-        d_all = done(sy.dma_start(T.allex[:], T.exall[:]), None, 16)
-        need(v, "v", d_all)
-        e_q = ev()
-        for e, q in ((0, T.eq0), (1, T.eq1)):
-            done(v.tensor_scalar(q[:], T.allex[:], float(2 * rank + e), None, Op.is_equal), e_q)
+        e_bs = done(v.tensor_scalar(T.mbs[:], T.rowg[:], gcol, None, Op.is_ge))
         need(v, "v", e_q)
         e_cnt = ev()
         for e, q in ((0, T.eq0), (1, T.eq1)):
             done(v.tensor_reduce(T.cnt[:, e:e + 1], q[:], AxisListType.X, Op.add), e_cnt)
-        need(t, "t", e_rc)
-        t.matmul(T.p5[:, 0:120], T.rd[0:16, :], T.pc[0:16, :], True, False)
-        need(t, "t", e_cnt)
-        t.matmul(T.p4[:, 0:2], T.rbs[:], T.cnt[:], True, True)
-        e_p4 = done(t.matmul(T.p4[:, 2:4], T.rb[:], T.cnt[:], True, True))
+        need(t, "t", e_cin)
+        t.matmul(T.p5[:, 0:120], T.rc[0:16, 0:128], T.rc[0:16, 188:308], True, False)
+        need(v, "v", e_cnt)
+        e_cb = done(v.tensor_copy(T.cntb[:], T.cnt[:]))
+        need(t, "t", e_bs, e_cb)
+        t.matmul(T.pb[:, 0:2], T.mbs[:], T.cntb[:], True, True)
+        e_p4 = done(t.matmul(T.pb[:, 2:4], T.mb[:], T.cntb[:], True, True))
         need(v, "v", e_p4)
-        e_wc = done(v.tensor_scalar(T.wc[:], T.p4[:, 2:4], -1.0, 512.0, Op.mult, Op.add))
-        need(v, "v", e_wc)
+        e_wc = done(v.tensor_scalar(T.wc[:], T.pb[:, 2:4], -1.0, 512.0, Op.mult, Op.add))
+        need(v, "v", e_wc, e_cin)
         e_u = ev()
         for e in range(2):
-            done(v.tensor_scalar(T.uu[:, 60 * e:60 * e + 60], T.pl[:], T.p4[:, e:e + 1], T.wc[:, e:e + 1], Op.is_ge, Op.mult), e_u)
+            done(v.tensor_scalar(T.uu[:, 60 * e:60 * e + 60], plc, T.pb[:, e:e + 1], T.wc[:, e:e + 1], Op.is_ge, Op.mult), e_u)
         need(t, "t", e_u)
-        e_p5 = done(t.matmul(T.p5[:, 0:120], T.rd[:], T.uu[:], False, True))
+        e_p5 = done(t.matmul(T.p5[:, 0:120], rd, T.uu[:], False, True))
         need(v, "v", e_p5)
         e_ro = done(v.tensor_scalar(T.roff[:], T.p5[:, 0:120], 4096.0, None, Op.min))
         arrived = [sem.arr, len(mine) * bits(m_off) + (len(his) - 1) * bits(m_off) + bits(m_on & ~m_off), "arr"]
         d_y, d_z = ev(), ev()
-        for h in range(2):
-            a, o = 480 * h, 30 * h
+        w = 960 // PIECES
+        for h in range(PIECES):
+            a, o, k = w * h, w // 16 * h, w // 16
             need(v, "v", e_ro, e_rc, arrived)
-            ea = done(v.tensor_copy(T.yt[:, a:a + 480], T.land[:, 0:4112].indirect(T.roff[:, o:o + 30])))
+            ea = done(v.tensor_copy(T.yt[:, a:a + w], T.land[:, 0:4112].indirect(T.roff[:, o:o + k])))
             need(s, "s", e_ro, e_rc, arrived)
-            eb = done(s.activation(T.yt[:, 960 + a:1440 + a], T.land[:, 0:4112].indirect(T.roff[:, 60 + o:90 + o]), Fn.Copy))
+            eb = done(s.activation(T.yt[:, 960 + a:960 + a + w], T.land[:, 0:4112].indirect(T.roff[:, 60 + o:60 + o + k]), Fn.Copy))
             need(sy, "y", ea)
-            done(sy.dma_start(T.y[:, a:a + 480], T.yt[:, a:a + 480]), d_y, 16)
-            q, nm, dd = (sy, "y", d_y) if h == 0 else (s, "s", d_z)
+            done(sy.dma_start(T.y[:, a:a + w], T.yt[:, a:a + w]), d_y, 16)
+            q, nm, dd = (sy, "y", d_y) if h < PIECES - 1 else (s, "s", d_z)
             need(q, nm, eb)
-            done(q.dma_start(T.y[:, 960 + a:1440 + a], T.yt[:, 960 + a:1440 + a]), dd, 16)
+            done(q.dma_start(T.y[:, 960 + a:960 + a + w], T.yt[:, 960 + a:960 + a + w]), dd, 16)
         need(sy, "y", d_y)
         need(s, "s", d_z)
     g.wait_ge(sem.ls, n_ls)

@@ -1,32 +1,34 @@
 from concourse.bass import DstId, RemoteDMATransfer
 from concourse.mybir import AluOpType as Op, AxisListType, ActivationFunctionType as Fn
 
-PIECES = 3
+X0 = 512
+PIECES = (((0, 480),), ((0, 224), (224, 480)))
 BF, F32, I32, U16 = "bfloat16", "float32", "int32", "uint16"
 SCRATCH = {
     "exall": ("dram", [8, 128, 16], I32),
     "e16": ("sbuf", [128, 128], I32), "e16b": ("sbuf", [128, 128], BF),
     "xs": ("sbuf", [128, 2048], BF), "sb": ("sbuf", [128, 2048], BF),
-    "land": ("sbuf", [128, 4112], BF), "yt": ("sbuf", [128, 1920], BF),
+    "l0": ("sbuf", [128, 2064], BF), "l1": ("sbuf", [128, 2064], BF), "yt": ("sbuf", [128, 1920], BF),
     "ci": ("sbuf", [128, 8], I32), "cf": ("sbuf", [128, 16], F32),
     "ka": ("sbuf", [128, 2], F32), "kcol": ("sbuf", [128, 2], F32),
     "rowi": ("sbuf", [128, 144], BF), "rowg": ("sbuf", [128, 128], BF), "row": ("sbuf", [128, 256], BF),
     "r16": ("sbuf", [128, 128], BF), "lneg": ("sbuf", [128, 128], BF), "lpos": ("sbuf", [128, 128], BF),
-    "mb": ("sbuf", [128, 128], BF), "mg": ("sbuf", [128, 128], BF), "mn": ("sbuf", [128, 128], BF), "mbs": ("sbuf", [128, 128], BF),
-    "zw": ("sbuf", [128, 240], BF), "zk": ("sbuf", [128, 240], BF), "zl": ("sbuf", [128, 144], BF),
+    "mb": ("sbuf", [128, 128], BF), "mg": ("sbuf", [128, 128], BF), "mbs": ("sbuf", [128, 128], BF),
+    "sg": ("sbuf", [128, 128], BF), "low": ("sbuf", [128, 128], BF),
+    "zw": ("sbuf", [128, 144], BF), "zk": ("sbuf", [128, 144], BF), "zl": ("sbuf", [128, 144], BF),
     "oh0": ("sbuf", [128, 128], BF), "pr0": ("sbuf", [128, 128], BF),
     "oh1": ("sbuf", [128, 128], BF), "pr1": ("sbuf", [128, 128], BF), "sc": ("sbuf", [128, 272], BF),
     "offs0": ("sbuf", [128, 16], U16), "offs1": ("sbuf", [128, 16], U16),
     "vals": ("sbuf", [128, 256], BF), "win": ("sbuf", [128, 2304], BF),
     "offx": ("sbuf", [128, 128], U16),
     "allex": ("sbuf", [128, 128], I32), "eq0": ("sbuf", [128, 128], F32), "eq1": ("sbuf", [128, 128], F32),
-    "cnt": ("sbuf", [128, 2], F32), "cntb": ("sbuf", [128, 2], BF), "rc": ("sbuf", [128, 308], F32),
+    "cnt": ("sbuf", [128, 2], F32), "cntb": ("sbuf", [128, 2], BF), "rc": ("sbuf", [128, 248], F32),
     "wc": ("sbuf", [128, 2], F32), "uu": ("sbuf", [128, 120], F32), "roff": ("sbuf", [128, 120], U16),
     "pb": ("psum", [128, 512], F32), "p10": ("psum", [128, 512], F32), "p11": ("psum", [128, 512], F32),
     "p20": ("psum", [128, 512], F32), "p21": ("psum", [128, 512], F32),
     "p3a": ("psum", [128, 512], F32), "p3b": ("psum", [128, 512], F32), "p5": ("psum", [128, 512], F32),
 }
-SEMAPHORES = ["cin", "xin", "oin", "exa", "arr", "ls"] + ["e%d" % k for k in range(80)]
+SEMAPHORES = ["cin", "xin", "oin", "exa", "arr0", "arr1", "rin0", "rin1", "ls"] + ["e%d" % k for k in range(95)]
 WORLD = 256
 
 
@@ -48,29 +50,45 @@ def plan(cores, topo):
             for d in range(n):
                 if z[d] == z[r] ^ dl:
                     (same if topo.same_plane(cores[r], cores[d]) else cross)[dl] = d
-        mine, his = [cross[1], same[2], same[3], mate], [cross[2], cross[3], same[1], r]
+        mine, his = [mate, cross[1], same[2], same[3]], [cross[2], cross[3], same[1], r]
         R = cores[r]
-        H = [c for c in range(WORLD) if c != R and topo.host(c) == topo.host(R) and topo.chip(c) == topo.chip(R)
-             and topo.die(c) != topo.die(R) and all(topo.may_write(c, cores[d]) for d in his)][0]
-        out.append((H, mine, his))
+        chip = [c for c in range(WORLD) if c != R and topo.host(c) == topo.host(R) and topo.chip(c) == topo.chip(R)]
+        H = [c for c in chip if topo.die(c) != topo.die(R) and all(topo.may_write(c, cores[d]) for d in his)][0]
+        Q = [c for c in chip if topo.die(c) == topo.die(R) and topo.may_write(c, cores[mate])][0]
+        out.append((H, mine, his, Q))
     return out
 
 
 def rank_program(g, core, T, topo):
     cores = list(T.cores)
     pl = plan(cores, topo)
+    sem = T.sem
+
+    def bits(m):
+        return bin(m).count("1")
+
     rank, helper = T.rank_of(core), False
     if rank is None:
+        for r in range(len(cores)):
+            if pl[r][3] == core:
+                d = cores[pl[r][1][0]]
+                m_off = topo.mask(core, d)
+                n_in = bits(topo.mask(cores[r], core) & ~m_off)
+                rid, pid = topo.addr(d, core)
+                for e, L in ((0, T.l0), (1, T.l1)):
+                    g.wait_ge(sem["rin%d" % e], n_in)
+                    g.remote_dma(L[:, 256 * r:256 * r + 256], T.sb[:, 1024 * e:1024 * e + 256], sem["arr%d" % e], sem.ls, pid, rid, m_off)
+                g.wait_ge(sem.ls, 2 * bits(m_off))
+                return
         own = [r for r in range(len(cores)) if pl[r][0] == core]
         if not own:
             return
         rank, helper = own[0], True
-    R, (H, mine, his) = cores[rank], pl[rank]
+    R, (H, mine, his, Q) = cores[rank], pl[rank]
     dests = his if helper else mine
     v, s, t, sy = g.vector, g.scalar, g.tensor, g.sync
-    sem = T.sem
     pcol, gi, ii, kp = [T.ci[:, k:k + 1] for k in range(4)]
-    gcol, icol, pf, kpf, kw, w0, w1, wg, ww = [T.cf[:, k:k + 1] for k in range(9)]
+    gcol, icol, kpf, kw, w0, w1, wg, ww, kw0 = [T.cf[:, k:k + 1] for k in range(9)]
     icol16 = T.cf[0:16, 1:2]
     rd, plc = T.rc[:, 0:128], T.rc[:, 128:188]
 
@@ -92,9 +110,6 @@ def rank_program(g, core, T, topo):
                 seen[(name, e[2])] = 1
                 q.wait_ge(e[0], e[1])
 
-    def bits(m):
-        return bin(m).count("1")
-
     far = [c for c in cores if topo.chip(c) != topo.chip(R) or topo.host(c) != topo.host(R)]
     m_off = topo.mask(core, far[0])
     m_on = topo.mask(core, R if helper else H)
@@ -103,16 +118,14 @@ def rank_program(g, core, T, topo):
     if not helper:
         d_ex = done(sy.dma_start(T.e16[0:16, :], T.ex[:]), None, 16)
         d_exd = done(s.dma_start(T.exall[rank], T.ex[:]), None, 16)
-        d_x0 = done(sy.dma_start(T.xs[:, 0:1024], T.x[:, 0:1024]), None, 16)
-        d_x1 = done(s.dma_start(T.xs[:, 1024:2048], T.x[:, 1024:2048]), None, 16)
+        d_x0 = done(sy.dma_start(T.xs[:, 0:X0], T.x[:, 0:X0]), None, 16)
+        d_x1 = done(sy.dma_start(T.xs[:, X0:2048], T.x[:, X0:2048]), None, 16)
 
     i_p = done(g.iota(pcol, [[0, 1]], 0, 1))
     i_i = done(g.iota(T.rowi[:], [[0, 9], [1, 16]], 0, 0, allow_small_or_imprecise_dtypes=True))
-    if not helper:
-        i_g = done(g.iota(T.rowg[:], [[1, 8], [0, 16]], 0, 0, allow_small_or_imprecise_dtypes=True))
-    i_r = done(g.iota(T.row[:], [[1, 256]], 0, 0, allow_small_or_imprecise_dtypes=True))
 
     if not helper:
+        i_g = done(g.iota(T.rowg[:], [[1, 8], [0, 16]], 0, 0, allow_small_or_imprecise_dtypes=True))
         rid_h, pid_h = topo.addr(H, core)
         need(g, "g", d_exd)
         ids = []
@@ -123,29 +136,35 @@ def rank_program(g, core, T, topo):
         g.remote_dma_fused([RemoteDMATransfer(dst_ids=ids, dma_engine_mask=m_off, remote_sem=sem.exa, srcs=[T.exall[rank]],
                                               dsts=[T.exall[rank] for d in ids])], local_sem=sem.ls)
         need(g, "g", d_x0)
-        g.remote_dma(T.xs[:, 0:1024], T.xs[:, 0:1024], sem.xin, sem.ls, pid_h, rid_h, m_on)
+        g.remote_dma(T.xs[:, 0:X0], T.xs[:, 0:X0], sem.xin, sem.ls, pid_h, rid_h, m_on)
         n_ls += bits(m_off) + bits(m_on)
+        i_r = done(g.iota(T.row[:], [[1, 256]], 0, 0, allow_small_or_imprecise_dtypes=True))
         xe = [d_x0, d_x1]
     else:
+        i_r = done(g.iota(T.row[:], [[1, 256]], 0, 0, allow_small_or_imprecise_dtypes=True))
         xe = [[sem.xin, 2 * bits(m_on), "xin"]]
 
+    e_k, e_ka = [], [ev(), ev()]
+
+    def experts(i, ds):
+        for k in range(4):
+            done(v.memset(T.ka[32 * k:32 * k + 32, i:i + 1], float(2 * ds[k])), e_ka[i])
+
+    def expert_column(i):
+        need(v, "v", e_ka[i], e_f2)
+        e_k.append(done(v.tensor_scalar(T.kcol[:, i:i + 1], T.ka[:, i:i + 1], kpf, None, Op.add)))
+
     if not helper:
-        e_ka = ev()
-        for i, ds in ((0, his), (1, mine)):
-            for k in range(4):
-                done(v.memset(T.ka[32 * k:32 * k + 32, i:i + 1], float(2 * ds[k])), e_ka)
+        experts(0, his)
         e_sz = done(v.memset(T.sc[:, 0:137:136], 0.0))
-        e_z0 = done(v.memset(T.zw[:], 0.0))
-        done(v.memset(T.zk[:], 0.0), e_z0)
     need(v, "v", i_p)
     e_c = done(v.tensor_scalar(gi, pcol, 4, None, Op.arith_shift_right))
     done(v.tensor_scalar(ii, pcol, 15, None, Op.bitwise_and), e_c)
     if not helper:
         done(v.tensor_scalar(kp, pcol, 4, 1, Op.arith_shift_right, Op.bitwise_and), e_c)
-        e_f2 = done(v.tensor_copy(pf, pcol))
     need(v, "v", e_c)
     e_f = done(v.tensor_copy(icol, ii))
-    done(v.tensor_copy(gcol, gi), e_f)
+    e_f2 = done(v.tensor_copy(gcol, gi))
     if not helper:
         done(v.tensor_copy(kpf, kp), e_f2)
     need(v, "v", e_f, i_i)
@@ -154,47 +173,62 @@ def rank_program(g, core, T, topo):
         e = done(v.tensor_scalar(w0, icol, 0.0, None, Op.is_equal))
         return done(v.tensor_scalar(w1, icol, 1.0, None, Op.is_equal), e)
 
-    def fold_matrix():
-        need(v, "v", e_w)
-        e_wg = done(v.tensor_scalar(wg, gcol, w1, 256.0, Op.mult, Op.mult))
+    def fold_a():
+        need(v, "v", e_w, e_f2)
+        return done(v.tensor_scalar(wg, gcol, w1, 256.0, Op.mult, Op.mult))
+
+    def fold_b():
         need(v, "v", e_wg)
-        e_ww = done(v.tensor_tensor(ww, w0, wg, Op.add))
+        return done(v.tensor_tensor(ww, w0, wg, Op.add))
+
+    def fold_c():
         need(v, "v", e_ww)
         return done(v.tensor_scalar(T.zl[:, 0:143], T.rowi[:, 0:143], 15.0, ww, Op.is_equal, Op.mult))
 
-    e_win, e_win2 = ev(), ev()
+    e_win0, e_win = ev(), ev()
+
+    def window():
+        done(v.memset(T.win[:, 1792:2304], 0.0), e_win)
+
     e_cin = [sem.cin, bits(m_on), "cin"]
     if helper:
         need(v, "v", i_r)
         e_rc = done(v.tensor_scalar(plc, T.row[:, 0:60], 16.0, icol, Op.mult, Op.add))
-        need(v, "v", e_rc)
+        done(v.tensor_scalar(T.rc[:, 188:248], T.row[:, 0:60], 16.0, icol, Op.mult, Op.add), e_rc)
         done(v.tensor_scalar(rd, T.rowi[:, 0:128], icol, None, Op.is_equal), e_rc)
-        done(v.tensor_copy(T.rc[:, 188:248], plc), e_rc)
-        done(v.tensor_scalar(T.rc[:, 248:308], plc, 256.0, None, Op.add), e_rc)
         need(g, "g", e_rc)
         rid, pid = topo.addr(R, core)
         g.remote_dma(T.rc[:], T.rc[:], sem.cin, sem.ls, pid, rid, m_on)
         n_ls += bits(m_on)
         e_w = col_weights()
-        e_zl = fold_matrix()
-        done(v.memset(T.win[:, 256:1280], 0.0), e_win)
+        e_wg = fold_a()
+        e_ww = fold_b()
+        e_zl = fold_c()
+        window()
         offs, e_of = T.offs0, [sem.oin, bits(m_on), "oin"]
+        need(s, "s", i_i)
     else:
         e_r16 = done(v.tensor_scalar(T.r16[0:16, :], T.rowi[0:16, 0:128], icol16, None, Op.is_equal))
-        need(v, "v", e_ka, e_f2)
-        e_k = done(v.tensor_scalar(T.kcol[:], T.ka[:], kpf, None, Op.add))
+        expert_column(0)
+        experts(1, mine)
         need(v, "v", i_g)
         e_b = done(v.tensor_scalar(T.mb[:], T.rowg[:], gcol, None, Op.is_equal))
-        done(v.tensor_scalar(T.mn[:], T.rowg[:], gcol, -1.0, Op.is_gt, Op.mult), e_b)
-        need(v, "v", i_r)
-        done(v.tensor_scalar(T.mg[:], T.row[:, 0:128], pf, None, Op.is_gt), e_b)
+        expert_column(1)
         need(s, "s", e_f, i_i)
         e_lp = done(s.activation(T.lpos[0:16, :], T.rowi[0:16, 0:128], Fn.Identity, bias=icol16, scale=16.0))
+        e_sg = done(s.activation(T.sg[:], T.rowi[:, 0:128], Fn.Sign, bias=icol, scale=-1.0))
         need(s, "s", e_lp)
         e_l = done(s.activation(T.lneg[0:16, :], T.lpos[0:16, :], Fn.Copy, scale=-1.0))
-    need(s, "s", i_r)
-    for k in range(4):
-        done(s.activation(T.win[:, 1280 + 256 * k:1536 + 256 * k], T.row[:], Fn.Copy, scale=0.0), e_win2)
+        need(s, "s", e_sg)
+        e_low = done(s.activation(T.low[:], T.sg[:], Fn.Relu, scale=-1.0))
+        e_z0 = ev()
+        for z in (T.zk, T.zw):
+            done(s.activation(z[:], T.rowi[:], Fn.Copy, scale=0.0), e_z0)
+    for a in range(256, 768, 128):
+        done(s.activation(T.win[:, a:a + 128], T.rowi[:, 0:128], Fn.Copy, scale=0.0), e_win0)
+    need(s, "s", e_win0)
+    for a in (768, 1280):
+        done(s.activation(T.win[:, a:a + 512], T.win[:, 256:768], Fn.Copy), e_win)
 
     if not helper:
         oh, pr, p1, p2, offs2 = (T.oh0, T.oh1), (T.pr0, T.pr1), (T.p10, T.p11), (T.p20, T.p21), (T.offs0, T.offs1)
@@ -206,52 +240,72 @@ def rank_program(g, core, T, topo):
         e_eb = done(v.tensor_copy(T.e16b[0:16, :], T.e16[0:16, :]))
         need(t, "t", e_eb)
         e_pb = done(t.matmul(T.pb[:, 0:128], T.r16[0:16, :], T.e16b[0:16, :], True, True))
-        e_w = col_weights()
-        e_kw = done(v.tensor_scalar(kw, gcol, 256.0, 256.0, Op.mult, Op.add))
-        need(v, "v", e_pb, e_k)
+        need(v, "v", e_low, e_b)
+        e_mg = done(v.tensor_tensor(T.mg[:], T.low[:], T.mb[:], Op.mult))
+        need(v, "v", e_pb)
         e_oh, e_sc = [], []
-        for i in range(2):
+
+        def one_hot(i):
+            need(v, "v", e_k[i])
             e_oh.append(done(v.tensor_scalar(oh[i][:], T.pb[:, 0:128], T.kcol[:, i:i + 1], None, Op.is_equal)))
+
+        def running_count(i):
             need(v, "v", e_oh[i], e_sz)
             e_sc.append(done(v.tensor_tensor_scan(T.sc[:, 136 * i + 1:136 * i + 129], oh[i][:], oh[i][:], 0.0, Op.add, Op.max)))
-            if i == 0:
-                need(v, "v", e_z0, e_kw)
-                e_zk = done(v.tensor_scalar(T.zk[:, 112:128], T.rowi[:, 0:16], icol, kw, Op.is_equal, Op.mult))
-                e_zw = done(v.tensor_scalar(T.zw[:, 112:128], T.rowi[:, 0:16], icol, None, Op.is_equal))
+
+        one_hot(0)
+        e_kw0 = done(v.tensor_scalar(kw0, kpf, 896.0, 256.0, Op.mult, Op.add))
+        running_count(0)
+        need(v, "v", e_kw0)
+        e_kw = done(v.tensor_scalar(kw, gcol, 128.0, kw0, Op.mult, Op.add))
+        need(v, "v", e_z0)
+        e_zw = done(v.tensor_scalar(T.zw[:, 64:80], T.rowi[:, 0:16], icol, None, Op.is_equal))
+        need(v, "v", e_kw)
+        e_zk = done(v.tensor_scalar(T.zk[:, 64:80], T.rowi[:, 0:16], icol, kw, Op.is_equal, Op.mult))
         for i in range(2):
-            need(t, "t", e_b, e_oh[i])
+            need(t, "t", e_mg, e_oh[i])
             t.matmul(p1[i][:, 0:128], T.mg[:], oh[i][:], False, False)
-            t.matmul(p1[i][:, 0:128], T.mn[:], oh[i][:], False, False)
-            need(t, "t", e_sz, e_sc[i])
+            need(t, "t", e_b, e_sz, e_sc[i])
             e_p1 = done(t.matmul(p1[i][:, 0:128], T.mb[:], T.sc[:, 136 * i:136 * i + 128], False, True))
             need(t, "t", e_zk)
             for k in range(8):
-                t.matmul(p2[i][:, 0:16], T.zk[:, 112 - 16 * k:240 - 16 * k], oh[i][:, 16 * k:16 * k + 16], False, False)
+                a, b = 32 * (k // 2), 64 - 16 * (k % 2)
+                t.matmul(p2[i][a:a + 32, 0:16], T.zk[:, b:b + 32], oh[i][:, 16 * k:16 * k + 16], False, False)
             need(v, "v", e_p1)
             e_pr = done(v.tensor_tensor(pr[i][:], p1[i][:, 0:128], oh[i][:], Op.mult))
             if i == 0:
-                e_zl = fold_matrix()
+                one_hot(1)
+                e_w = col_weights()
+                running_count(1)
             else:
-                done(v.memset(T.win[:, 256:1280], 0.0), e_win)
+                e_ww = fold_b()
+                window()
+                e_zl = fold_c()
             need(t, "t", e_zw, e_pr)
             for k in range(8):
-                ins = t.matmul(p2[i][:, 0:16], T.zw[:, 112 - 16 * k:240 - 16 * k], pr[i][:, 16 * k:16 * k + 16], False, k == 7)
+                a, b = 32 * (k // 2), 64 - 16 * (k % 2)
+                ins = t.matmul(p2[i][a:a + 32, 0:16], T.zw[:, b:b + 32], pr[i][:, 16 * k:16 * k + 16], False, k % 2 == 1)
             e_p2 = done(ins)
             need(v, "v", e_p2)
             e_of = done(v.tensor_copy(offs2[i][:], p2[i][:, 0:16]))
             if i == 0:
+                e_wg = fold_a()
                 need(g, "g", e_of)
                 g.remote_dma(T.offs0[:], T.offs0[:], sem.oin, sem.ls, pid_h, rid_h, m_on)
                 need(g, "g", d_x1)
-                g.remote_dma(T.xs[:, 1024:2048], T.xs[:, 1024:2048], sem.xin, sem.ls, pid_h, rid_h, m_on)
+                g.remote_dma(T.xs[:, X0:2048], T.xs[:, X0:2048], sem.xin, sem.ls, pid_h, rid_h, m_on)
                 n_ls += 2 * bits(m_on)
         offs = T.offs1
 
-    need(s, "s", e_w)
+    need(s, "s", e_w, i_r)
     e_vals = done(s.activation(T.vals[:], T.row[:], Fn.Identity, bias=w1, scale=w0))
-    need(v, "v", e_of, e_win, e_win2, e_vals)
+    need(v, "v", e_of, e_win0, e_win, e_vals)
     e_sct = done(v.tensor_copy(T.win[:, 0:2304].indirect(offs[:, 0:16]), T.vals[:]))
-    need(t, "t", e_zl, e_win, e_win2, e_sct)
+    if not helper:
+        e_z = done(v.memset(T.l0[:, 2048:2064], 0.0))
+        done(v.memset(T.l1[:, 2048:2064], 0.0), e_z)
+        e_bs = done(v.tensor_scalar(T.mbs[:], T.rowg[:], gcol, None, Op.is_ge))
+    need(t, "t", e_zl, e_win0, e_win, e_sct)
     e_p3 = []
     for b, P in ((0, T.p3a), (1, T.p3b)):
         for lo in range(16):
@@ -259,50 +313,49 @@ def rank_program(g, core, T, topo):
             ins = t.matmul(P[:, 0:64], T.zl[:, 15 - lo:143 - lo], T.win[:, a:a + 1009:16], lo == 0, lo == 15)
         e_p3.append(done(ins))
 
-    e_ox, e_gv, e_gs, e_q = [], [], [], ev()
-
-    def conv(b):
-        need(v, "v", e_p3[b])
-        e_ox.append(done(v.tensor_copy(T.offx[:, 64 * b:64 * b + 64], (T.p3a, T.p3b)[b][:, 0:64])))
-
-    conv(0)
-    for k in range(4):
-        if k == 2:
-            if not helper:
-                need(sy, "y", d_exd, [sem.exa, (len(cores) - 1) * bits(m_off), "exa"])
-                d_all = done(sy.dma_start(T.allex[:], T.exall[:]), None, 16)
-                need(v, "v", d_all)
-                for e, q in ((0, T.eq0), (1, T.eq1)):
-                    done(v.tensor_scalar(q[:], T.allex[:], float(2 * rank + e), None, Op.is_equal), e_q)
-            conv(1)
-        need(v, "v", e_ox[k // 2], *xe)
-        c, o = 512 * k, 32 * k
-        e_gv.append(done(v.tensor_copy(T.sb[:, c:c + 256], T.xs[:, 0:2048].indirect(T.offx[:, o:o + 16]))))
-        need(s, "s", e_ox[k // 2], *xe)
-        e_gs.append(done(s.activation(T.sb[:, c + 256:c + 512], T.xs[:, 0:2048].indirect(T.offx[:, o + 16:o + 32]), Fn.Copy)))
-        need(g, "g", e_gv[k], e_gs[k])
-        d = cores[dests[k]]
-        rid, pid = topo.addr(d, core)
-        m = m_on & ~m_off if d == R else topo.mask(core, d)
-        g.remote_dma(T.land[:, 512 * rank:512 * rank + 512], T.sb[:, c:c + 512], sem.arr, sem.ls, pid, rid, m)
-        n_ls += bits(m)
+    for e, P, L in ((0, T.p3a, T.l0), (1, T.p3b, T.l1)):
+        need(v, "v", e_p3[e])
+        e_ox = done(v.tensor_copy(T.offx[:, 64 * e:64 * e + 64], P[:, 0:64]))
+        for h in range(2):
+            c, o = 1024 * e + 512 * h, 64 * e + 32 * h
+            need(v, "v", e_ox, *xe)
+            e_gv = done(v.tensor_copy(T.sb[:, c:c + 256], T.xs[:, 0:2048].indirect(T.offx[:, o:o + 16])))
+            need(s, "s", e_ox, *xe)
+            e_gs = done(s.activation(T.sb[:, c + 256:c + 512], T.xs[:, 0:2048].indirect(T.offx[:, o + 16:o + 32]), Fn.Copy))
+            for k, e_g in ((2 * h, e_gv), (2 * h + 1, e_gs)):
+                b = 1024 * e + 256 * k
+                need(g, "g", e_g)
+                if k == 0 and not helper:
+                    m = topo.mask(core, Q) & ~m_off
+                    rid, pid = topo.addr(Q, core)
+                    g.remote_dma(T.sb[:, b:b + 256], T.sb[:, b:b + 256], sem["rin%d" % e], sem.ls, pid, rid, m)
+                else:
+                    d = cores[dests[k]]
+                    m = m_on & ~m_off if d == R else topo.mask(core, d)
+                    rid, pid = topo.addr(d, core)
+                    g.remote_dma(L[:, 256 * rank:256 * rank + 256], T.sb[:, b:b + 256], sem["arr%d" % e], sem.ls, pid, rid, m)
+                n_ls += bits(m)
 
     if not helper:
-        e_rc = done(v.memset(T.land[:, 4096:4112], 0.0))
-        e_bs = done(v.tensor_scalar(T.mbs[:], T.rowg[:], gcol, None, Op.is_ge))
+        need(sy, "y", d_exd, [sem.exa, (len(cores) - 1) * bits(m_off), "exa"])
+        d_all = done(sy.dma_start(T.allex[:], T.exall[:]), None, 16)
+        need(v, "v", d_all)
+        e_q = ev()
+        for e, q in ((0, T.eq0), (1, T.eq1)):
+            done(v.tensor_scalar(q[:], T.allex[:], float(2 * rank + e), None, Op.is_equal), e_q)
         need(v, "v", e_q)
         e_cnt = ev()
         for e, q in ((0, T.eq0), (1, T.eq1)):
             done(v.tensor_reduce(T.cnt[:, e:e + 1], q[:], AxisListType.X, Op.add), e_cnt)
         need(t, "t", e_cin)
-        t.matmul(T.p5[:, 0:120], T.rc[0:16, 0:128], T.rc[0:16, 188:308], True, False)
+        t.matmul(T.p5[:, 0:120], T.rc[0:16, 0:128], T.rc[0:16, 128:248], True, False)
         need(v, "v", e_cnt)
         e_cb = done(v.tensor_copy(T.cntb[:], T.cnt[:]))
         need(t, "t", e_bs, e_cb)
         t.matmul(T.pb[:, 0:2], T.mbs[:], T.cntb[:], True, True)
         e_p4 = done(t.matmul(T.pb[:, 2:4], T.mb[:], T.cntb[:], True, True))
         need(v, "v", e_p4)
-        e_wc = done(v.tensor_scalar(T.wc[:], T.pb[:, 2:4], -1.0, 512.0, Op.mult, Op.add))
+        e_wc = done(v.tensor_scalar(T.wc[:], T.pb[:, 2:4], -1.0, 256.0, Op.mult, Op.add))
         need(v, "v", e_wc, e_cin)
         e_u = ev()
         for e in range(2):
@@ -310,21 +363,22 @@ def rank_program(g, core, T, topo):
         need(t, "t", e_u)
         e_p5 = done(t.matmul(T.p5[:, 0:120], rd, T.uu[:], False, True))
         need(v, "v", e_p5)
-        e_ro = done(v.tensor_scalar(T.roff[:], T.p5[:, 0:120], 4096.0, None, Op.min))
-        arrived = [sem.arr, len(mine) * bits(m_off) + (len(his) - 1) * bits(m_off) + bits(m_on & ~m_off), "arr"]
+        e_ro = done(v.tensor_scalar(T.roff[:], T.p5[:, 0:120], 2048.0, None, Op.min))
+        n_arr = (len(mine) + len(his) - 1) * bits(m_off) + bits(m_on & ~m_off)
         d_y, d_z = ev(), ev()
-        w = 960 // PIECES
-        for h in range(PIECES):
-            a, o, k = w * h, w // 16 * h, w // 16
-            need(v, "v", e_ro, e_rc, arrived)
-            ea = done(v.tensor_copy(T.yt[:, a:a + w], T.land[:, 0:4112].indirect(T.roff[:, o:o + k])))
-            need(s, "s", e_ro, e_rc, arrived)
-            eb = done(s.activation(T.yt[:, 960 + a:960 + a + w], T.land[:, 0:4112].indirect(T.roff[:, 60 + o:60 + o + k]), Fn.Copy))
-            need(sy, "y", ea)
-            done(sy.dma_start(T.y[:, a:a + w], T.yt[:, a:a + w]), d_y, 16)
-            q, nm, dd = (sy, "y", d_y) if h < PIECES - 1 else (s, "s", d_z)
-            need(q, nm, eb)
-            done(q.dma_start(T.y[:, 960 + a:960 + a + w], T.yt[:, 960 + a:960 + a + w]), dd, 16)
+        for e, L in ((0, T.l0), (1, T.l1)):
+            arrived = [sem["arr%d" % e], n_arr, "arr%d" % e]
+            for lo, hi in PIECES[e]:
+                a, b, o, w = 960 * e + lo, 960 * e + 480 + lo, 60 * e + lo // 16, hi - lo
+                need(v, "v", e_ro, e_z, arrived)
+                ea = done(v.tensor_copy(T.yt[:, a:a + w], L[:, 0:2064].indirect(T.roff[:, o:o + w // 16])))
+                need(s, "s", e_ro, e_z, arrived)
+                eb = done(s.activation(T.yt[:, b:b + w], L[:, 0:2064].indirect(T.roff[:, o + 30:o + 30 + w // 16]), Fn.Copy))
+                need(sy, "y", ea)
+                done(sy.dma_start(T.y[:, a:a + w], T.yt[:, a:a + w]), d_y, 16)
+                q, nm, dd = (s, "s", d_z) if e == 1 and hi == 480 else (sy, "y", d_y)
+                need(q, nm, eb)
+                done(q.dma_start(T.y[:, b:b + w], T.yt[:, b:b + w]), dd, 16)
         need(sy, "y", d_y)
         need(s, "s", d_z)
     g.wait_ge(sem.ls, n_ls)

from concourse.bass import DstId, RemoteDMATransfer
from concourse.mybir import AluOpType as Op, AxisListType, ActivationFunctionType as Fn

X0 = 512
PIECES = (((0, 480),), ((0, 224), (224, 480)))
BF, F32, I32, U16 = "bfloat16", "float32", "int32", "uint16"
SCRATCH = {
    "exall": ("dram", [8, 128, 16], I32),
    "e16": ("sbuf", [128, 128], I32), "e16b": ("sbuf", [128, 128], BF),
    "xs": ("sbuf", [128, 2048], BF), "sb": ("sbuf", [128, 2048], BF),
    "l0": ("sbuf", [128, 2064], BF), "l1": ("sbuf", [128, 2064], BF), "yt": ("sbuf", [128, 1920], BF),
    "ci": ("sbuf", [128, 8], I32), "cf": ("sbuf", [128, 16], F32),
    "ka": ("sbuf", [128, 2], F32), "kcol": ("sbuf", [128, 2], F32),
    "rowi": ("sbuf", [128, 144], BF), "rowg": ("sbuf", [128, 128], BF), "row": ("sbuf", [128, 256], BF),
    "r16": ("sbuf", [128, 128], BF), "lneg": ("sbuf", [128, 128], BF), "lpos": ("sbuf", [128, 128], BF),
    "mb": ("sbuf", [128, 128], BF), "mg": ("sbuf", [128, 128], BF), "mbs": ("sbuf", [128, 128], BF),
    "sg": ("sbuf", [128, 128], BF), "low": ("sbuf", [128, 128], BF),
    "zw": ("sbuf", [128, 144], BF), "zk": ("sbuf", [128, 144], BF), "zl": ("sbuf", [128, 144], BF),
    "oh0": ("sbuf", [128, 128], BF), "pr0": ("sbuf", [128, 128], BF),
    "oh1": ("sbuf", [128, 128], BF), "pr1": ("sbuf", [128, 128], BF), "sc": ("sbuf", [128, 272], BF),
    "offs0": ("sbuf", [128, 16], U16), "offs1": ("sbuf", [128, 16], U16),
    "vals": ("sbuf", [128, 256], BF), "win": ("sbuf", [128, 2304], BF),
    "offx": ("sbuf", [128, 128], U16),
    "allex": ("sbuf", [128, 128], I32), "eq0": ("sbuf", [128, 128], F32), "eq1": ("sbuf", [128, 128], F32),
    "cnt": ("sbuf", [128, 2], F32), "cntb": ("sbuf", [128, 2], BF), "rc": ("sbuf", [128, 248], F32),
    "wc": ("sbuf", [128, 2], F32), "uu": ("sbuf", [128, 120], F32), "roff": ("sbuf", [128, 120], U16),
    "pb": ("psum", [128, 512], F32), "p10": ("psum", [128, 512], F32), "p11": ("psum", [128, 512], F32),
    "p20": ("psum", [128, 512], F32), "p21": ("psum", [128, 512], F32),
    "p3a": ("psum", [128, 512], F32), "p3b": ("psum", [128, 512], F32), "p5": ("psum", [128, 512], F32),
}
SEMAPHORES = ["cin", "xin", "oin", "exa", "arr0", "arr1", "rin0", "rin1", "ls"] + ["e%d" % k for k in range(95)]
WORLD = 256


def plan(cores, topo):
    n = len(cores)
    lead, z = [], []
    for r in range(n):
        m = [q for q in range(r) if topo.mates(cores[r], cores[q])]
        if m:
            z.append(z[m[0]])
        else:
            z.append(len(lead))
            lead.append(r)
    out = []
    for r in range(n):
        mate = [d for d in range(n) if d != r and topo.mates(cores[r], cores[d])][0]
        same, cross = {}, {}
        for dl in range(1, len(lead)):
            for d in range(n):
                if z[d] == z[r] ^ dl:
                    (same if topo.same_plane(cores[r], cores[d]) else cross)[dl] = d
        mine, his = [mate, cross[1], same[2], same[3]], [cross[2], cross[3], same[1], r]
        R = cores[r]
        chip = [c for c in range(WORLD) if c != R and topo.host(c) == topo.host(R) and topo.chip(c) == topo.chip(R)]
        H = [c for c in chip if topo.die(c) != topo.die(R) and all(topo.may_write(c, cores[d]) for d in his)][0]
        Q = [c for c in chip if topo.die(c) == topo.die(R) and topo.may_write(c, cores[mate])][0]
        out.append((H, mine, his, Q))
    return out


def rank_program(g, core, T, topo):
    cores = list(T.cores)
    pl = plan(cores, topo)
    sem = T.sem

    def bits(m):
        return bin(m).count("1")

    rank, helper = T.rank_of(core), False
    if rank is None:
        for r in range(len(cores)):
            if pl[r][3] == core:
                d = cores[pl[r][1][0]]
                m_off = topo.mask(core, d)
                n_in = bits(topo.mask(cores[r], core) & ~m_off)
                rid, pid = topo.addr(d, core)
                for e, L in ((0, T.l0), (1, T.l1)):
                    g.wait_ge(sem["rin%d" % e], n_in)
                    g.remote_dma(L[:, 256 * r:256 * r + 256], T.sb[:, 1024 * e:1024 * e + 256], sem["arr%d" % e], sem.ls, pid, rid, m_off)
                g.wait_ge(sem.ls, 2 * bits(m_off))
                return
        own = [r for r in range(len(cores)) if pl[r][0] == core]
        if not own:
            return
        rank, helper = own[0], True
    R, (H, mine, his, Q) = cores[rank], pl[rank]
    dests = his if helper else mine
    v, s, t, sy = g.vector, g.scalar, g.tensor, g.sync
    pcol, gi, ii, kp = [T.ci[:, k:k + 1] for k in range(4)]
    gcol, icol, kpf, kw, w0, w1, wg, ww, kw0 = [T.cf[:, k:k + 1] for k in range(9)]
    icol16 = T.cf[0:16, 1:2]
    rd, plc = T.rc[:, 0:128], T.rc[:, 128:188]

    used, seen = [0], {}

    def ev():
        used[0] += 1
        return [sem["e%d" % (used[0] - 1)], 0, used[0]]

    def done(ins, e=None, n=1):
        e = e or ev()
        ins.then_inc(e[0], n)
        e[1] += n
        return e

    def need(q, name, *es):
        for e in es:
            if (name, e[2]) not in seen:
                seen[(name, e[2])] = 1
                q.wait_ge(e[0], e[1])

    far = [c for c in cores if topo.chip(c) != topo.chip(R) or topo.host(c) != topo.host(R)]
    m_off = topo.mask(core, far[0])
    m_on = topo.mask(core, R if helper else H)
    n_ls = 0

    if not helper:
        d_ex = done(sy.dma_start(T.e16[0:16, :], T.ex[:]), None, 16)
        d_exd = done(s.dma_start(T.exall[rank], T.ex[:]), None, 16)
        d_x0 = done(sy.dma_start(T.xs[:, 0:X0], T.x[:, 0:X0]), None, 16)
        d_x1 = done(sy.dma_start(T.xs[:, X0:2048], T.x[:, X0:2048]), None, 16)

    i_p = done(g.iota(pcol, [[0, 1]], 0, 1))
    i_i = done(g.iota(T.rowi[:], [[0, 9], [1, 16]], 0, 0, allow_small_or_imprecise_dtypes=True))

    if not helper:
        i_g = done(g.iota(T.rowg[:], [[1, 8], [0, 16]], 0, 0, allow_small_or_imprecise_dtypes=True))
        rid_h, pid_h = topo.addr(H, core)
        need(g, "g", d_exd)
        ids = []
        for d in range(len(cores)):
            if d != rank:
                rid, pid = topo.addr(cores[d], core)
                ids.append(DstId(rid=rid, pnc=pid))
        g.remote_dma_fused([RemoteDMATransfer(dst_ids=ids, dma_engine_mask=m_off, remote_sem=sem.exa, srcs=[T.exall[rank]],
                                              dsts=[T.exall[rank] for d in ids])], local_sem=sem.ls)
        need(g, "g", d_x0)
        g.remote_dma(T.xs[:, 0:X0], T.xs[:, 0:X0], sem.xin, sem.ls, pid_h, rid_h, m_on)
        n_ls += bits(m_off) + bits(m_on)
        i_r = done(g.iota(T.row[:], [[1, 256]], 0, 0, allow_small_or_imprecise_dtypes=True))
        xe = [d_x0, d_x1]
    else:
        i_r = done(g.iota(T.row[:], [[1, 256]], 0, 0, allow_small_or_imprecise_dtypes=True))
        xe = [[sem.xin, 2 * bits(m_on), "xin"]]

    e_k, e_ka = [], [ev(), ev()]

    def experts(i, ds):
        for k in range(4):
            done(v.memset(T.ka[32 * k:32 * k + 32, i:i + 1], float(2 * ds[k])), e_ka[i])

    def expert_column(i):
        need(v, "v", e_ka[i], e_f2)
        e_k.append(done(v.tensor_scalar(T.kcol[:, i:i + 1], T.ka[:, i:i + 1], kpf, None, Op.add)))

    if not helper:
        experts(0, his)
        e_sz = done(v.memset(T.sc[:, 0:137:136], 0.0))
    need(v, "v", i_p)
    e_c = done(v.tensor_scalar(gi, pcol, 4, None, Op.arith_shift_right))
    done(v.tensor_scalar(ii, pcol, 15, None, Op.bitwise_and), e_c)
    if not helper:
        done(v.tensor_scalar(kp, pcol, 4, 1, Op.arith_shift_right, Op.bitwise_and), e_c)
    need(v, "v", e_c)
    e_f = done(v.tensor_copy(icol, ii))
    e_f2 = done(v.tensor_copy(gcol, gi))
    if not helper:
        done(v.tensor_copy(kpf, kp), e_f2)
    need(v, "v", e_f, i_i)

    def col_weights():
        e = done(v.tensor_scalar(w0, icol, 0.0, None, Op.is_equal))
        return done(v.tensor_scalar(w1, icol, 1.0, None, Op.is_equal), e)

    def fold_a():
        need(v, "v", e_w, e_f2)
        return done(v.tensor_scalar(wg, gcol, w1, 256.0, Op.mult, Op.mult))

    def fold_b():
        need(v, "v", e_wg)
        return done(v.tensor_tensor(ww, w0, wg, Op.add))

    def fold_c():
        need(v, "v", e_ww)
        return done(v.tensor_scalar(T.zl[:, 0:143], T.rowi[:, 0:143], 15.0, ww, Op.is_equal, Op.mult))

    e_win0, e_win = ev(), ev()

    def window():
        done(v.memset(T.win[:, 1792:2304], 0.0), e_win)

    e_cin = [sem.cin, bits(m_on), "cin"]
    if helper:
        need(v, "v", i_r)
        e_rc = done(v.tensor_scalar(plc, T.row[:, 0:60], 16.0, icol, Op.mult, Op.add))
        done(v.tensor_scalar(T.rc[:, 188:248], T.row[:, 0:60], 16.0, icol, Op.mult, Op.add), e_rc)
        done(v.tensor_scalar(rd, T.rowi[:, 0:128], icol, None, Op.is_equal), e_rc)
        need(g, "g", e_rc)
        rid, pid = topo.addr(R, core)
        g.remote_dma(T.rc[:], T.rc[:], sem.cin, sem.ls, pid, rid, m_on)
        n_ls += bits(m_on)
        e_w = col_weights()
        e_wg = fold_a()
        e_ww = fold_b()
        e_zl = fold_c()
        window()
        offs, e_of = T.offs0, [sem.oin, bits(m_on), "oin"]
        need(s, "s", i_i)
    else:
        e_r16 = done(v.tensor_scalar(T.r16[0:16, :], T.rowi[0:16, 0:128], icol16, None, Op.is_equal))
        expert_column(0)
        experts(1, mine)
        need(v, "v", i_g)
        e_b = done(v.tensor_scalar(T.mb[:], T.rowg[:], gcol, None, Op.is_equal))
        expert_column(1)
        need(s, "s", e_f, i_i)
        e_lp = done(s.activation(T.lpos[0:16, :], T.rowi[0:16, 0:128], Fn.Identity, bias=icol16, scale=16.0))
        e_sg = done(s.activation(T.sg[:], T.rowi[:, 0:128], Fn.Sign, bias=icol, scale=-1.0))
        need(s, "s", e_lp)
        e_l = done(s.activation(T.lneg[0:16, :], T.lpos[0:16, :], Fn.Copy, scale=-1.0))
        need(s, "s", e_sg)
        e_low = done(s.activation(T.low[:], T.sg[:], Fn.Relu, scale=-1.0))
        e_z0 = ev()
        for z in (T.zk, T.zw):
            done(s.activation(z[:], T.rowi[:], Fn.Copy, scale=0.0), e_z0)
    for a in range(256, 768, 128):
        done(s.activation(T.win[:, a:a + 128], T.rowi[:, 0:128], Fn.Copy, scale=0.0), e_win0)
    need(s, "s", e_win0)
    for a in (768, 1280):
        done(s.activation(T.win[:, a:a + 512], T.win[:, 256:768], Fn.Copy), e_win)

    if not helper:
        oh, pr, p1, p2, offs2 = (T.oh0, T.oh1), (T.pr0, T.pr1), (T.p10, T.p11), (T.p20, T.p21), (T.offs0, T.offs1)
        need(t, "t", e_r16, e_lp, e_l)
        for i in range(2):
            t.matmul(p1[i][:, 0:128], T.r16[0:16, :], T.lneg[0:16, :], True, False)
            t.matmul(p2[i][:, 0:16], T.r16[0:16, :], T.lpos[0:16, 0:16], True, False)
        need(v, "v", d_ex)
        e_eb = done(v.tensor_copy(T.e16b[0:16, :], T.e16[0:16, :]))
        need(t, "t", e_eb)
        e_pb = done(t.matmul(T.pb[:, 0:128], T.r16[0:16, :], T.e16b[0:16, :], True, True))
        need(v, "v", e_low, e_b)
        e_mg = done(v.tensor_tensor(T.mg[:], T.low[:], T.mb[:], Op.mult))
        need(v, "v", e_pb)
        e_oh, e_sc = [], []

        def one_hot(i):
            need(v, "v", e_k[i])
            e_oh.append(done(v.tensor_scalar(oh[i][:], T.pb[:, 0:128], T.kcol[:, i:i + 1], None, Op.is_equal)))

        def running_count(i):
            need(v, "v", e_oh[i], e_sz)
            e_sc.append(done(v.tensor_tensor_scan(T.sc[:, 136 * i + 1:136 * i + 129], oh[i][:], oh[i][:], 0.0, Op.add, Op.max)))

        one_hot(0)
        e_kw0 = done(v.tensor_scalar(kw0, kpf, 896.0, 256.0, Op.mult, Op.add))
        running_count(0)
        need(v, "v", e_kw0)
        e_kw = done(v.tensor_scalar(kw, gcol, 128.0, kw0, Op.mult, Op.add))
        need(v, "v", e_z0)
        e_zw = done(v.tensor_scalar(T.zw[:, 64:80], T.rowi[:, 0:16], icol, None, Op.is_equal))
        need(v, "v", e_kw)
        e_zk = done(v.tensor_scalar(T.zk[:, 64:80], T.rowi[:, 0:16], icol, kw, Op.is_equal, Op.mult))
        for i in range(2):
            need(t, "t", e_mg, e_oh[i])
            t.matmul(p1[i][:, 0:128], T.mg[:], oh[i][:], False, False)
            need(t, "t", e_b, e_sz, e_sc[i])
            e_p1 = done(t.matmul(p1[i][:, 0:128], T.mb[:], T.sc[:, 136 * i:136 * i + 128], False, True))
            need(t, "t", e_zk)
            for k in range(8):
                a, b = 32 * (k // 2), 64 - 16 * (k % 2)
                t.matmul(p2[i][a:a + 32, 0:16], T.zk[:, b:b + 32], oh[i][:, 16 * k:16 * k + 16], False, False)
            need(v, "v", e_p1)
            e_pr = done(v.tensor_tensor(pr[i][:], p1[i][:, 0:128], oh[i][:], Op.mult))
            if i == 0:
                one_hot(1)
                e_w = col_weights()
                running_count(1)
            else:
                e_ww = fold_b()
                window()
                e_zl = fold_c()
            need(t, "t", e_zw, e_pr)
            for k in range(8):
                a, b = 32 * (k // 2), 64 - 16 * (k % 2)
                ins = t.matmul(p2[i][a:a + 32, 0:16], T.zw[:, b:b + 32], pr[i][:, 16 * k:16 * k + 16], False, k % 2 == 1)
            e_p2 = done(ins)
            need(v, "v", e_p2)
            e_of = done(v.tensor_copy(offs2[i][:], p2[i][:, 0:16]))
            if i == 0:
                e_wg = fold_a()
                need(g, "g", e_of)
                g.remote_dma(T.offs0[:], T.offs0[:], sem.oin, sem.ls, pid_h, rid_h, m_on)
                need(g, "g", d_x1)
                g.remote_dma(T.xs[:, X0:2048], T.xs[:, X0:2048], sem.xin, sem.ls, pid_h, rid_h, m_on)
                n_ls += 2 * bits(m_on)
        offs = T.offs1

    need(s, "s", e_w, i_r)
    e_vals = done(s.activation(T.vals[:], T.row[:], Fn.Identity, bias=w1, scale=w0))
    need(v, "v", e_of, e_win0, e_win, e_vals)
    e_sct = done(v.tensor_copy(T.win[:, 0:2304].indirect(offs[:, 0:16]), T.vals[:]))
    if not helper:
        e_z = done(v.memset(T.l0[:, 2048:2064], 0.0))
        done(v.memset(T.l1[:, 2048:2064], 0.0), e_z)
        e_bs = done(v.tensor_scalar(T.mbs[:], T.rowg[:], gcol, None, Op.is_ge))
    need(t, "t", e_zl, e_win0, e_win, e_sct)
    e_p3 = []
    for b, P in ((0, T.p3a), (1, T.p3b)):
        for lo in range(16):
            a = 256 + 1024 * b + lo
            ins = t.matmul(P[:, 0:64], T.zl[:, 15 - lo:143 - lo], T.win[:, a:a + 1009:16], lo == 0, lo == 15)
        e_p3.append(done(ins))

    for e, P, L in ((0, T.p3a, T.l0), (1, T.p3b, T.l1)):
        need(v, "v", e_p3[e])
        e_ox = done(v.tensor_copy(T.offx[:, 64 * e:64 * e + 64], P[:, 0:64]))
        for h in range(2):
            c, o = 1024 * e + 512 * h, 64 * e + 32 * h
            need(v, "v", e_ox, *xe)
            e_gv = done(v.tensor_copy(T.sb[:, c:c + 256], T.xs[:, 0:2048].indirect(T.offx[:, o:o + 16])))
            need(s, "s", e_ox, *xe)
            e_gs = done(s.activation(T.sb[:, c + 256:c + 512], T.xs[:, 0:2048].indirect(T.offx[:, o + 16:o + 32]), Fn.Copy))
            for k, e_g in ((2 * h, e_gv), (2 * h + 1, e_gs)):
                b = 1024 * e + 256 * k
                need(g, "g", e_g)
                if k == 0 and not helper:
                    m = topo.mask(core, Q) & ~m_off
                    rid, pid = topo.addr(Q, core)
                    g.remote_dma(T.sb[:, b:b + 256], T.sb[:, b:b + 256], sem["rin%d" % e], sem.ls, pid, rid, m)
                else:
                    d = cores[dests[k]]
                    m = m_on & ~m_off if d == R else topo.mask(core, d)
                    rid, pid = topo.addr(d, core)
                    g.remote_dma(L[:, 256 * rank:256 * rank + 256], T.sb[:, b:b + 256], sem["arr%d" % e], sem.ls, pid, rid, m)
                n_ls += bits(m)

    if not helper:
        need(sy, "y", d_exd, [sem.exa, (len(cores) - 1) * bits(m_off), "exa"])
        d_all = done(sy.dma_start(T.allex[:], T.exall[:]), None, 16)
        need(v, "v", d_all)
        e_q = ev()
        for e, q in ((0, T.eq0), (1, T.eq1)):
            done(v.tensor_scalar(q[:], T.allex[:], float(2 * rank + e), None, Op.is_equal), e_q)
        need(v, "v", e_q)
        e_cnt = ev()
        for e, q in ((0, T.eq0), (1, T.eq1)):
            done(v.tensor_reduce(T.cnt[:, e:e + 1], q[:], AxisListType.X, Op.add), e_cnt)
        need(t, "t", e_cin)
        t.matmul(T.p5[:, 0:120], T.rc[0:16, 0:128], T.rc[0:16, 128:248], True, False)
        need(v, "v", e_cnt)
        e_cb = done(v.tensor_copy(T.cntb[:], T.cnt[:]))
        need(t, "t", e_bs, e_cb)
        t.matmul(T.pb[:, 0:2], T.mbs[:], T.cntb[:], True, True)
        e_p4 = done(t.matmul(T.pb[:, 2:4], T.mb[:], T.cntb[:], True, True))
        need(v, "v", e_p4)
        e_wc = done(v.tensor_scalar(T.wc[:], T.pb[:, 2:4], -1.0, 256.0, Op.mult, Op.add))
        need(v, "v", e_wc, e_cin)
        e_u = ev()
        for e in range(2):
            done(v.tensor_scalar(T.uu[:, 60 * e:60 * e + 60], plc, T.pb[:, e:e + 1], T.wc[:, e:e + 1], Op.is_ge, Op.mult), e_u)
        need(t, "t", e_u)
        e_p5 = done(t.matmul(T.p5[:, 0:120], rd, T.uu[:], False, True))
        need(v, "v", e_p5)
        e_ro = done(v.tensor_scalar(T.roff[:], T.p5[:, 0:120], 2048.0, None, Op.min))
        n_arr = (len(mine) + len(his) - 1) * bits(m_off) + bits(m_on & ~m_off)
        d_y, d_z = ev(), ev()
        for e, L in ((0, T.l0), (1, T.l1)):
            arrived = [sem["arr%d" % e], n_arr, "arr%d" % e]
            for lo, hi in PIECES[e]:
                a, b, o, w = 960 * e + lo, 960 * e + 480 + lo, 60 * e + lo // 16, hi - lo
                need(v, "v", e_ro, e_z, arrived)
                ea = done(v.tensor_copy(T.yt[:, a:a + w], L[:, 0:2064].indirect(T.roff[:, o:o + w // 16])))
                need(s, "s", e_ro, e_z, arrived)
                eb = done(s.activation(T.yt[:, b:b + w], L[:, 0:2064].indirect(T.roff[:, o + 30:o + 30 + w // 16]), Fn.Copy))
                need(sy, "y", ea)
                done(sy.dma_start(T.y[:, a:a + w], T.yt[:, a:a + w]), d_y, 16)
                q, nm, dd = (s, "s", d_z) if e == 1 and hi == 480 else (sy, "y", d_y)
                need(q, nm, eb)
                done(q.dma_start(T.y[:, b:b + w], T.yt[:, b:b + w]), dd, 16)
        need(sy, "y", d_y)
        need(s, "s", d_z)
    g.wait_ge(sem.ls, n_ls)
